import numpy as np
import ml_dtypes


def mxq(x, axis, fmt="e4m3"):
    dtype, down = {"e4m3": (ml_dtypes.float8_e4m3fn, 7), "e5m2": (ml_dtypes.float8_e5m2, 14)}[fmt]
    v = np.moveaxis(np.asarray(x, np.float32).astype(ml_dtypes.bfloat16).astype(np.float64), axis, -1)
    blocks = v.reshape(v.shape[:-1] + (-1, 32))
    amax = np.abs(blocks).max(-1, keepdims=True)
    byte = np.maximum(np.where(amax > 0, np.frexp(amax)[1] - 1 + 127, 0) - down, 1)
    scale = np.exp2(byte - 127.0)
    codes = (blocks / scale).astype(np.float32).astype(dtype).astype(np.float64)
    return np.moveaxis((codes * scale).reshape(v.shape), -1, axis)


WIDE = False


def mx_kscale(k):
    if not WIDE:
        return np.ones(k)
    levels = np.array([30, -30])
    if k % 512:
        return np.exp2(np.random.permutation(np.resize(levels, k // 32))).repeat(32)
    a = np.empty((k // 512, 16))
    for p in range(k // 512):
        a[p, :8] = np.random.permutation(np.resize(levels, 8))
        for g in range(8):
            far = levels[np.abs(levels - a[p, g]) >= 10]
            a[p, g + 8] = far[np.random.randint(len(far))]
    return np.exp2(a.ravel()).repeat(32)


def f64(x):
    return np.asarray(x).astype(np.float64)


E2M1 = np.array([0.0, 0.5, 1.0, 1.5, 2.0, 3.0, 4.0, 6.0, -0.0, -0.5, -1.0, -1.5, -2.0, -3.0, -4.0, -6.0])


def pack_weight(w, fmt):
    k, n = w.shape
    w = f64(np.asarray(w, np.float32).astype(ml_dtypes.bfloat16)).reshape(k // 32, 32, n)
    amax = np.abs(w).max(1)
    if fmt == "e4m3":
        byte = np.frexp(amax)[1] - 1 + 127 - 7
    else:
        mant, ex = np.frexp(amax / 6.0)
        byte = np.where(mant > 0.5, ex, ex - 1) + 127
    byte = np.clip(np.where(amax > 0, byte, 1), 1, 254)
    scaled = (w * np.exp2(127.0 - byte)[:, None, :]).reshape(k, n).astype(np.float32)
    by_word = np.ascontiguousarray(scaled.reshape(k // 512, 128, 4, n).transpose(0, 1, 3, 2))
    if fmt == "e4m3":
        words = by_word.astype(ml_dtypes.float8_e4m3fn).view(np.uint8)
    else:
        c = by_word.astype(ml_dtypes.float4_e2m1fn).view(np.uint8) & 0xF
        words = (c[..., 0::2] | (c[..., 1::2] << 4)).reshape(k // 512, 128, 2 * n)
    return np.ascontiguousarray(words), np.ascontiguousarray(byte.astype(np.uint8).reshape(k // 512, 16, n))


def unpack_weight(words, scales, fmt):
    g, _, n = scales.shape
    words = np.ascontiguousarray(words).reshape(g, 128, n, -1)
    if fmt == "e4m3":
        vals = words.view(ml_dtypes.float8_e4m3fn).astype(np.float64)
    else:
        nib = np.empty((g, 128, n, 4), np.uint8)
        nib[..., 0::2] = words & 0xF
        nib[..., 1::2] = words >> 4
        vals = E2M1[nib]
    vals = vals * np.repeat(np.exp2(scales.astype(np.float64) - 127.0), 8, axis=1)[..., None]
    return vals.transpose(0, 1, 3, 2).reshape(g * 512, n)


def planes(y):
    n, m = y.shape
    v = y.astype(np.float32).astype(ml_dtypes.bfloat16).astype(np.float64).reshape(n // 32, 32, m)
    top = np.abs(v).max(1)
    byte = np.clip(np.where(top > 0, np.frexp(top)[1] - 1 + 127 - 7, 1), 1, 254)
    codes = (v * np.exp2(127.0 - byte)[:, None, :]).reshape(n, m).astype(np.float32).astype(ml_dtypes.float8_e4m3fn).view(np.uint8)
    words = codes.reshape(n // 512, 128, 4, m).transpose(0, 1, 3, 2)
    return np.ascontiguousarray(words), np.ascontiguousarray(byte.astype(np.uint8).reshape(n // 512, 16, m))


O, K, M, T = 512, 2560, 512, 512


def setup_inputs():
    n = np.random.standard_normal
    s = mx_kscale(K)[:, None]
    dy = np.exp(0.5 * n((1, T))) * n((K, T))
    w = n((K, M)) / np.sqrt(K) / s
    p_w8 = pack_weight(w[:O], "e4m3")
    p_w4 = pack_weight(w[O:], "e2m1")
    return {
        "dy": (dy * s).astype(np.float32),
        "w8_words": p_w8[0],
        "w8_scales": p_w8[1],
        "w4_words": p_w4[0],
        "w4_scales": p_w4[1],
        "g": (n((512, 512))).astype(np.float32),
    }


def reference(dy, w8_words, w8_scales, w4_words, w4_scales, g):
    dy_ = mxq(f64(dy), 0, "e5m2")
    w8_ = unpack_weight(w8_words, w8_scales, "e4m3")
    w4_ = unpack_weight(w4_words, w4_scales, "e2m1")
    y = w8_.T @ dy_[:O] + w4_.T @ dy_[O:]
    out_0 = f64(g) * y
    return (out_0,) + planes(out_0)

@@ -1,0 +1,212 @@
+from contextlib import ExitStack
+
+import concourse.mybir as mybir
+from concourse.masks import make_identity
+
+O, K, D, T = 512, 2560, 512, 512
+FLOPS = 2 * K * D * T
+
+F32 = mybir.dt.float32
+BF16 = mybir.dt.bfloat16
+I32 = mybir.dt.int32
+U32 = mybir.dt.uint32
+U8 = mybir.dt.uint8
+E4M3 = mybir.dt.float8_e4m3fn_x4
+E5M2 = mybir.dt.float8_e5m2_x4
+E2M1 = mybir.dt.float4_e2m1fn_x4
+MULT = mybir.AluOpType.mult
+
+P = 128
+PACK = 4
+K_PASS = P * PACK
+PASSES = K // K_PASS
+TB = 128
+BLOCKS = T // TB
+HALF = T // 2
+SCALAR_COLS = 192
+
+
+def tile_mix_dyq_fm_pl_mul_kernel(
+    tc, dy, w8_words, w8_scales, w4_words, w4_scales, g, out_0, out_1, out_2
+):
+    nc = tc.nc
+    with ExitStack() as ctx:
+        sb = ctx.enter_context(tc.tile_pool(name="sb", bufs=1))
+        ps = ctx.enter_context(tc.psum_pool(name="ps", bufs=1))
+        ctx.enter_context(tc.manual_schedule())
+
+        w8 = sb.tile([P, D], U32, name="w8", align_bytes=64)
+        w4 = sb.tile([P, PASSES - 1, 2 * D], U8, name="w4", align_bytes=64)
+        w4_sc = sb.tile([P, PASSES - 1, D], U8, name="w4_sc", align_bytes=64)
+        w8_sc = sb.tile([P, D], U8, name="w8_sc", align_bytes=64)
+        ident = sb.tile([P, P], F32, name="ident", align_bytes=64)
+        dy_codes = [sb.tile([P, T], U32, name=f"dy_codes{a}", align_bytes=64) for a in range(PASSES)]
+        dy_sc = [sb.tile([P, T], U8, name=f"dy_sc{a}", align_bytes=64) for a in range(PASSES)]
+        dy_bf = [sb.tile([P, T, PACK], BF16, name=f"dy_bf{a}", align_bytes=64) for a in range(PASSES)]
+        out_codes = sb.tile([P, T], U32, name="out_codes", align_bytes=64)
+        out_sc = sb.tile([P, T], U8, name="out_sc", align_bytes=64)
+        acc = [ps.tile([P, D], F32, name=f"acc{b}") for b in range(BLOCKS)]
+        flip = [ps.tile([P, PACK, TB], F32, name=f"flip{b}") for b in range(BLOCKS)]
+        dealt = [sb.tile([P, PACK, P], F32, name=f"dealt{b}", align_bytes=64) for b in range(BLOCKS)]
+        out_bf = [sb.tile([P, TB, PACK], BF16, name=f"out_bf{b}", align_bytes=64) for b in range(BLOCKS)]
+
+        def by_partition(rows):
+            return rows.rearrange("(p j) w -> p j w", j=PACK)
+
+        def load(src, t0, t1, name):
+            raw = sb.tile([P, PACK, t1 - t0], F32, name=name, align_bytes=64)
+            nc.sync.dma_start(out=raw[:], in_=by_partition(src)[:, :, t0:t1])
+            return raw
+
+        def dy_rows(a):
+            return dy[a * K_PASS : (a + 1) * K_PASS, :]
+
+        nc.vector.memset(w4_sc[:].rearrange("p a n -> p (a n)").bitcast(I32), 0)
+        nc.vector.memset(w8_sc[:].bitcast(I32), 0)
+        make_identity(nc, ident[:])
+
+        def load_w4_scales():
+            for q in range(4):
+                nc.sync.dma_start(
+                    out=w4_sc[32 * q : 32 * q + 4, :, :].bitcast(I32),
+                    in_=w4_scales[:, 4 * q : 4 * q + 4, :].rearrange("a r n -> r a n").bitcast(I32),
+                )
+
+        def load_w8_scales():
+            for q in range(4):
+                nc.sync.dma_start(
+                    out=w8_sc[32 * q : 32 * q + 4, :].bitcast(I32),
+                    in_=w8_scales[0, 4 * q : 4 * q + 4, :].bitcast(I32),
+                )
+
+        raw = {}
+        raw[1] = load(dy_rows(1), 0, T, "raw1")
+        nc.sync.dma_start(out=w4[:].bitcast(I32), in_=w4_words.rearrange("a p n -> p a n").bitcast(I32))
+        raw[2] = load(dy_rows(2), 0, T, "raw2")
+        load_w4_scales()
+        raw[3] = load(dy_rows(3), 0, T, "raw3")
+        load_w8_scales()
+        raw[4] = load(dy_rows(4), 0, T, "raw4")
+        last_h0 = load(dy_rows(0), 0, HALF, "last_h0")
+        nc.sync.dma_start(out=w8[:].bitcast(I32), in_=w8_words[0].rearrange("p n t -> p (n t)").bitcast(I32))
+        last_b2 = load(dy_rows(0), 2 * TB, 3 * TB, "last_b2")
+        last_b3 = load(dy_rows(0), 3 * TB, 4 * TB, "last_b3")
+        g_half = [load(g, h * HALF, (h + 1) * HALF, f"g{h}") for h in range(2)]
+        last = [last_h0[:, :, 0:TB], last_h0[:, :, TB:HALF], last_b2[:], last_b3[:]]
+
+        out_h0 = sb.tile([P, PACK, HALF], F32, name="out_h0", align_bytes=64)
+        out_b2 = sb.tile([P, PACK, TB], F32, name="out_b2", align_bytes=64)
+        out_b3 = sb.tile([P, PACK, TB], F32, name="out_b3", align_bytes=64)
+        out_f = [out_h0[:, :, 0:TB], out_h0[:, :, TB:HALF], out_b2[:], out_b3[:]]
+
+        def cast_scalar(dst, src):
+            nc.scalar.copy(out=dst, in_=src.rearrange("p j w -> p w j"))
+
+        def cast_vector(dst, src):
+            nc.vector.tensor_copy(out=dst, in_=src.rearrange("p j w -> p w j"))
+
+        def quant_dy(a, t0, t1):
+            nc.vector.quantize_mx(
+                out=dy_codes[a][:, t0:t1].bitcast(E5M2),
+                scales=dy_sc[a][:, t0:t1],
+                in_=dy_bf[a][:, t0:t1, :].rearrange("p w j -> p (w j)"),
+            )
+
+        def product(a, b):
+            cols = slice(b * TB, (b + 1) * TB)
+            if a == 0:
+                rhs, rhs_scale = w8[:].bitcast(E4M3), w8_sc[:]
+            else:
+                rhs, rhs_scale = w4[:, a - 1, :].bitcast(E2M1), w4_sc[:, a - 1, :]
+            nc.tensor.matmul_mx(
+                out=acc[b][:],
+                lhsT=dy_codes[a][:, cols].bitcast(E5M2),
+                lhsT_scale=dy_sc[a][:, cols],
+                rhs=rhs,
+                rhs_scale=rhs_scale,
+                start=(a == 1),
+                stop=(a == 0),
+            )
+
+        def deal(b):
+            nc.scalar.copy(out=dealt[b][:], in_=acc[b][:].rearrange("t (m i) -> t i m", i=PACK))
+
+        def turn(b):
+            for i in range(PACK):
+                nc.tensor.transpose(flip[b][:, i, :], dealt[b][:, i, :], ident[:])
+
+        def gate(b):
+            h, r = divmod(b, 2)
+            nc.vector.tensor_tensor(
+                out=out_f[b], in0=flip[b][:], in1=g_half[h][:, :, r * TB : (r + 1) * TB], op=MULT
+            )
+
+        def quant_out(b):
+            cols = slice(b * TB, (b + 1) * TB)
+            nc.vector.quantize_mx(
+                out=out_codes[:, cols].bitcast(E4M3),
+                scales=out_sc[:, cols],
+                in_=out_bf[b][:].rearrange("p w j -> p (w j)"),
+            )
+
+        def store_out(src, t0, t1):
+            nc.sync.dma_start(out=by_partition(out_0)[:, :, t0:t1], in_=src)
+
+        def store_codes(t0, t1):
+            words = out_1[0].rearrange("p t i -> p (t i)").bitcast(I32)
+            nc.sync.dma_start(out=words[:, t0:t1], in_=out_codes[:, t0:t1].bitcast(I32))
+
+        for a in range(1, PASSES):
+            cast_scalar(dy_bf[a][:, 0:SCALAR_COLS, :], raw[a][:, :, 0:SCALAR_COLS])
+            cast_vector(dy_bf[a][:, SCALAR_COLS:T, :], raw[a][:, :, SCALAR_COLS:T])
+            quant_dy(a, 0, T)
+            for b in range(BLOCKS):
+                product(a, b)
+
+        def blk(b):
+            return dy_bf[0][:, b * TB : (b + 1) * TB, :]
+
+        cast_scalar(blk(0), last[0])
+        cast_vector(blk(1), last[1])
+        quant_dy(0, 0, TB)
+        quant_dy(0, TB, HALF)
+        product(0, 0)
+        product(0, 1)
+        deal(0)
+        cast_vector(blk(2), last[2])
+        quant_dy(0, 2 * TB, 3 * TB)
+        turn(0)
+        deal(1)
+        product(0, 2)
+        cast_vector(blk(3), last[3])
+        quant_dy(0, 3 * TB, 4 * TB)
+        turn(1)
+        deal(2)
+        product(0, 3)
+        deal(3)
+        turn(2)
+        turn(3)
+
+        gate(0)
+        cast_scalar(out_bf[0][:], out_f[0])
+        gate(1)
+        store_out(out_h0[:], 0, HALF)
+        cast_scalar(out_bf[1][:], out_f[1])
+        gate(2)
+        store_out(out_b2[:], 2 * TB, 3 * TB)
+        cast_scalar(out_bf[2][:], out_f[2])
+        gate(3)
+        store_out(out_b3[:], 3 * TB, 4 * TB)
+        quant_out(0)
+        cast_vector(out_bf[3][:], out_f[3])
+        quant_out(1)
+        store_codes(0, HALF)
+        quant_out(2)
+        quant_out(3)
+        store_codes(HALF, T)
+        for q in range(4):
+            eng = nc.scalar if q % 2 == 0 else nc.sync
+            eng.dma_start(
+                out=out_2[0, 4 * q : 4 * q + 4, :].bitcast(I32),
+                in_=out_sc[32 * q : 32 * q + 4, :].bitcast(I32),
+            )

@@ -67,28 +67,29 @@ def tile_mix_dyq_fm_pl_mul_kernel(
 
         def load_w4_scales():
             for q in range(4):
-                nc.sync.dma_start(
-                    out=w4_sc[32 * q : 32 * q + 4, :, :].bitcast(I32),
-                    in_=w4_scales[:, 4 * q : 4 * q + 4, :].rearrange("a r n -> r a n").bitcast(I32),
+                nc.scalar.dma_start(
+                    out=w4_sc[q:P:32, :, :].bitcast(I32),
+                    in_=w4_scales[:, q:16:4, :].rearrange("a r n -> r a n").bitcast(I32),
                 )
 
         def load_w8_scales():
             for q in range(4):
                 nc.sync.dma_start(
-                    out=w8_sc[32 * q : 32 * q + 4, :].bitcast(I32),
-                    in_=w8_scales[0, 4 * q : 4 * q + 4, :].bitcast(I32),
+                    out=w8_sc[q:P:32, :].bitcast(I32),
+                    in_=w8_scales[0, q:16:4, :].bitcast(I32),
                 )
 
         raw = {}
         raw[1] = load(dy_rows(1), 0, T, "raw1")
         nc.sync.dma_start(out=w4[:].bitcast(I32), in_=w4_words.rearrange("a p n -> p a n").bitcast(I32))
-        raw[2] = load(dy_rows(2), 0, T, "raw2")
         load_w4_scales()
+        raw[2] = load(dy_rows(2), 0, T, "raw2")
         raw[3] = load(dy_rows(3), 0, T, "raw3")
-        load_w8_scales()
-        raw[4] = load(dy_rows(4), 0, T, "raw4")
+        prev_h0 = load(dy_rows(4), 0, HALF, "prev_h0")
         last_h0 = load(dy_rows(0), 0, HALF, "last_h0")
+        load_w8_scales()
         nc.sync.dma_start(out=w8[:].bitcast(I32), in_=w8_words[0].rearrange("p n t -> p (n t)").bitcast(I32))
+        prev_h1 = load(dy_rows(4), HALF, T, "prev_h1")
         last_b2 = load(dy_rows(0), 2 * TB, 3 * TB, "last_b2")
         last_b3 = load(dy_rows(0), 3 * TB, 4 * TB, "last_b3")
         g_half = [load(g, h * HALF, (h + 1) * HALF, f"g{h}") for h in range(2)]
@@ -156,36 +157,47 @@ def tile_mix_dyq_fm_pl_mul_kernel(
             words = out_1[0].rearrange("p t i -> p (t i)").bitcast(I32)
             nc.sync.dma_start(out=words[:, t0:t1], in_=out_codes[:, t0:t1].bitcast(I32))
 
-        for a in range(1, PASSES):
+        for a in range(1, PASSES - 1):
             cast_scalar(dy_bf[a][:, 0:SCALAR_COLS, :], raw[a][:, :, 0:SCALAR_COLS])
             cast_vector(dy_bf[a][:, SCALAR_COLS:T, :], raw[a][:, :, SCALAR_COLS:T])
             quant_dy(a, 0, T)
             for b in range(BLOCKS):
                 product(a, b)
 
-        def blk(b):
-            return dy_bf[0][:, b * TB : (b + 1) * TB, :]
+        def blk(a, b):
+            return dy_bf[a][:, b * TB : (b + 1) * TB, :]
 
-        cast_scalar(blk(0), last[0])
-        cast_vector(blk(1), last[1])
-        quant_dy(0, 0, TB)
-        quant_dy(0, TB, HALF)
-        product(0, 0)
-        product(0, 1)
+        for a, src in ((4, prev_h0), (0, last_h0)):
+            cast_scalar(blk(a, 0), src[:, :, 0:TB])
+            cast_vector(blk(a, 1), src[:, :, TB:HALF])
+            quant_dy(a, 0, TB)
+            quant_dy(a, TB, HALF)
+            product(a, 0)
+            product(a, 1)
         deal(0)
-        cast_vector(blk(2), last[2])
-        quant_dy(0, 2 * TB, 3 * TB)
-        turn(0)
         deal(1)
-        product(0, 2)
-        cast_vector(blk(3), last[3])
-        quant_dy(0, 3 * TB, 4 * TB)
+        turn(0)
         turn(1)
+        cast_vector(dy_bf[4][:, HALF:T, :], prev_h1[:])
+        cast_vector(blk(0, 2), last[2])
+        cast_scalar(blk(0, 3), last[3])
+        quant_dy(4, HALF, T)
+        quant_dy(0, 2 * TB, 3 * TB)
+        quant_dy(0, 3 * TB, 4 * TB)
+        for b in (2, 3):
+            product(4, b)
+            product(0, b)
         deal(2)
-        product(0, 3)
-        deal(3)
         turn(2)
-        turn(3)
+        spare = acc[0][:].rearrange("p (i t) -> p i t", i=PACK)
+        banks3 = (flip[3][:], spare)
+        for u in range(2):
+            nc.scalar.copy(
+                out=dealt[3][:, 2 * u : 2 * u + 2, :],
+                in_=acc[3][:].rearrange("t (m i) -> t i m", i=PACK)[:, 2 * u : 2 * u + 2, :],
+            )
+            for i in (2 * u, 2 * u + 1):
+                nc.tensor.transpose(banks3[u][:, i, :], dealt[3][:, i, :], ident[:])
 
         gate(0)
         cast_scalar(out_bf[0][:], out_f[0])
@@ -195,7 +207,13 @@ def tile_mix_dyq_fm_pl_mul_kernel(
         gate(2)
         store_out(out_b2[:], 2 * TB, 3 * TB)
         cast_scalar(out_bf[2][:], out_f[2])
-        gate(3)
+        for u in range(2):
+            nc.vector.tensor_tensor(
+                out=out_b3[:, 2 * u : 2 * u + 2, :],
+                in0=banks3[u][:, 2 * u : 2 * u + 2, :],
+                in1=g_half[1][:, 2 * u : 2 * u + 2, TB:HALF],
+                op=MULT,
+            )
         store_out(out_b3[:], 3 * TB, 4 * TB)
         quant_out(0)
         cast_vector(out_bf[3][:], out_f[3])

@@ -67,7 +67,7 @@ def tile_mix_dyq_fm_pl_mul_kernel(
 
         def load_w4_scales():
             for q in range(4):
-                nc.scalar.dma_start(
+                nc.sync.dma_start(
                     out=w4_sc[q:P:32, :, :].bitcast(I32),
                     in_=w4_scales[:, q:16:4, :].rearrange("a r n -> r a n").bitcast(I32),
                 )
@@ -81,30 +81,32 @@ def tile_mix_dyq_fm_pl_mul_kernel(
 
         raw = {}
         raw[1] = load(dy_rows(1), 0, T, "raw1")
-        nc.sync.dma_start(out=w4[:].bitcast(I32), in_=w4_words.rearrange("a p n -> p a n").bitcast(I32))
         load_w4_scales()
+        nc.sync.dma_start(out=w4[:].bitcast(I32), in_=w4_words.rearrange("a p n -> p a n").bitcast(I32))
         raw[2] = load(dy_rows(2), 0, T, "raw2")
-        raw[3] = load(dy_rows(3), 0, T, "raw3")
+        third_h0 = load(dy_rows(3), 0, HALF, "third_h0")
+        load_w8_scales()
         prev_h0 = load(dy_rows(4), 0, HALF, "prev_h0")
         last_h0 = load(dy_rows(0), 0, HALF, "last_h0")
-        load_w8_scales()
         nc.sync.dma_start(out=w8[:].bitcast(I32), in_=w8_words[0].rearrange("p n t -> p (n t)").bitcast(I32))
-        prev_h1 = load(dy_rows(4), HALF, T, "prev_h1")
+        third_h1 = load(dy_rows(3), HALF, T, "third_h1")
+        prev_b2 = load(dy_rows(4), 2 * TB, 3 * TB, "prev_b2")
         last_b2 = load(dy_rows(0), 2 * TB, 3 * TB, "last_b2")
+        prev_b3 = load(dy_rows(4), 3 * TB, 4 * TB, "prev_b3")
         last_b3 = load(dy_rows(0), 3 * TB, 4 * TB, "last_b3")
-        g_half = [load(g, h * HALF, (h + 1) * HALF, f"g{h}") for h in range(2)]
-        last = [last_h0[:, :, 0:TB], last_h0[:, :, TB:HALF], last_b2[:], last_b3[:]]
+        g_blk = [load(g, b * TB, (b + 1) * TB, f"g_b{b}")[:] for b in range(BLOCKS)]
 
-        out_h0 = sb.tile([P, PACK, HALF], F32, name="out_h0", align_bytes=64)
-        out_b2 = sb.tile([P, PACK, TB], F32, name="out_b2", align_bytes=64)
-        out_b3 = sb.tile([P, PACK, TB], F32, name="out_b3", align_bytes=64)
-        out_f = [out_h0[:, :, 0:TB], out_h0[:, :, TB:HALF], out_b2[:], out_b3[:]]
+        out_f = [sb.tile([P, PACK, TB], F32, name=f"out_b{b}", align_bytes=64)[:] for b in range(BLOCKS)]
 
         def cast_scalar(dst, src):
-            nc.scalar.copy(out=dst, in_=src.rearrange("p j w -> p w j"))
+            nc.scalar.copy(
+                out=dst.rearrange("p (c i) j -> p c j i", i=4), in_=src.rearrange("p j (c i) -> p c j i", i=4)
+            )
 
         def cast_vector(dst, src):
-            nc.vector.tensor_copy(out=dst, in_=src.rearrange("p j w -> p w j"))
+            nc.vector.tensor_copy(
+                out=dst.rearrange("p (c i) j -> p c j i", i=4), in_=src.rearrange("p j (c i) -> p c j i", i=4)
+            )
 
         def quant_dy(a, t0, t1):
             nc.vector.quantize_mx(
@@ -137,10 +139,7 @@ def tile_mix_dyq_fm_pl_mul_kernel(
                 nc.tensor.transpose(flip[b][:, i, :], dealt[b][:, i, :], ident[:])
 
         def gate(b):
-            h, r = divmod(b, 2)
-            nc.vector.tensor_tensor(
-                out=out_f[b], in0=flip[b][:], in1=g_half[h][:, :, r * TB : (r + 1) * TB], op=MULT
-            )
+            nc.vector.tensor_tensor(out=out_f[b], in0=flip[b][:], in1=g_blk[b], op=MULT)
 
         def quant_out(b):
             cols = slice(b * TB, (b + 1) * TB)
@@ -157,64 +156,81 @@ def tile_mix_dyq_fm_pl_mul_kernel(
             words = out_1[0].rearrange("p t i -> p (t i)").bitcast(I32)
             nc.sync.dma_start(out=words[:, t0:t1], in_=out_codes[:, t0:t1].bitcast(I32))
 
-        for a in range(1, PASSES - 1):
+        def blk(a, b):
+            return dy_bf[a][:, b * TB : (b + 1) * TB, :]
+
+        def quant_blk(a, b):
+            quant_dy(a, b * TB, (b + 1) * TB)
+
+        spare = acc[0][:].rearrange("p (i t) -> p i t", i=PACK)
+        banks3 = (flip[3][:], spare)
+
+        def deal_turn_last():
+            for u in range(2):
+                nc.scalar.copy(
+                    out=dealt[3][:, 2 * u : 2 * u + 2, :],
+                    in_=acc[3][:].rearrange("t (m i) -> t i m", i=PACK)[:, 2 * u : 2 * u + 2, :],
+                )
+                for i in (2 * u, 2 * u + 1):
+                    nc.tensor.transpose(banks3[u][:, i, :], dealt[3][:, i, :], ident[:])
+
+        def gate_last():
+            for u in range(2):
+                nc.vector.tensor_tensor(
+                    out=out_f[3][:, 2 * u : 2 * u + 2, :],
+                    in0=banks3[u][:, 2 * u : 2 * u + 2, :],
+                    in1=g_blk[3][:, 2 * u : 2 * u + 2, :],
+                    op=MULT,
+                )
+
+        for a in range(1, PASSES - 2):
             cast_scalar(dy_bf[a][:, 0:SCALAR_COLS, :], raw[a][:, :, 0:SCALAR_COLS])
             cast_vector(dy_bf[a][:, SCALAR_COLS:T, :], raw[a][:, :, SCALAR_COLS:T])
             quant_dy(a, 0, T)
             for b in range(BLOCKS):
                 product(a, b)
 
-        def blk(a, b):
-            return dy_bf[a][:, b * TB : (b + 1) * TB, :]
-
-        for a, src in ((4, prev_h0), (0, last_h0)):
+        for a, src in ((3, third_h0), (4, prev_h0), (0, last_h0)):
             cast_scalar(blk(a, 0), src[:, :, 0:TB])
             cast_vector(blk(a, 1), src[:, :, TB:HALF])
-            quant_dy(a, 0, TB)
-            quant_dy(a, TB, HALF)
+            quant_blk(a, 0)
+            quant_blk(a, 1)
             product(a, 0)
             product(a, 1)
         deal(0)
         deal(1)
         turn(0)
+        cast_vector(dy_bf[3][:, HALF:T, :], third_h1[:])
+        cast_vector(blk(4, 2), prev_b2[:])
+        quant_dy(3, HALF, T)
+        cast_vector(blk(0, 2), last_b2[:])
+        quant_blk(4, 2)
+        cast_scalar(blk(4, 3), prev_b3[:])
+        quant_blk(0, 2)
         turn(1)
-        cast_vector(dy_bf[4][:, HALF:T, :], prev_h1[:])
-        cast_vector(blk(0, 2), last[2])
-        cast_scalar(blk(0, 3), last[3])
-        quant_dy(4, HALF, T)
-        quant_dy(0, 2 * TB, 3 * TB)
-        quant_dy(0, 3 * TB, 4 * TB)
-        for b in (2, 3):
-            product(4, b)
-            product(0, b)
+        product(3, 2)
+        product(4, 2)
+        product(0, 2)
+        product(3, 3)
         deal(2)
+        cast_vector(blk(0, 3), last_b3[:])
+        quant_blk(4, 3)
+        quant_blk(0, 3)
+        product(4, 3)
+        product(0, 3)
         turn(2)
-        spare = acc[0][:].rearrange("p (i t) -> p i t", i=PACK)
-        banks3 = (flip[3][:], spare)
-        for u in range(2):
-            nc.scalar.copy(
-                out=dealt[3][:, 2 * u : 2 * u + 2, :],
-                in_=acc[3][:].rearrange("t (m i) -> t i m", i=PACK)[:, 2 * u : 2 * u + 2, :],
-            )
-            for i in (2 * u, 2 * u + 1):
-                nc.tensor.transpose(banks3[u][:, i, :], dealt[3][:, i, :], ident[:])
-
         gate(0)
+        store_out(out_f[0], 0, TB)
+        deal_turn_last()
         cast_scalar(out_bf[0][:], out_f[0])
         gate(1)
-        store_out(out_h0[:], 0, HALF)
+        store_out(out_f[1], TB, HALF)
         cast_scalar(out_bf[1][:], out_f[1])
         gate(2)
-        store_out(out_b2[:], 2 * TB, 3 * TB)
+        store_out(out_f[2], 2 * TB, 3 * TB)
         cast_scalar(out_bf[2][:], out_f[2])
-        for u in range(2):
-            nc.vector.tensor_tensor(
-                out=out_b3[:, 2 * u : 2 * u + 2, :],
-                in0=banks3[u][:, 2 * u : 2 * u + 2, :],
-                in1=g_half[1][:, 2 * u : 2 * u + 2, TB:HALF],
-                op=MULT,
-            )
-        store_out(out_b3[:], 3 * TB, 4 * TB)
+        gate_last()
+        store_out(out_f[3], 3 * TB, 4 * TB)
         quant_out(0)
         cast_vector(out_bf[3][:], out_f[3])
         quant_out(1)

@@ -3,7 +3,7 @@ from contextlib import ExitStack
 import concourse.mybir as mybir
 from concourse.masks import make_identity
 
-O, K, D, T = 512, 2560, 512, 512
+K, D, T = 2560, 512, 512
 FLOPS = 2 * K * D * T
 
 F32 = mybir.dt.float32
@@ -14,16 +14,19 @@ U8 = mybir.dt.uint8
 E4M3 = mybir.dt.float8_e4m3fn_x4
 E5M2 = mybir.dt.float8_e5m2_x4
 E2M1 = mybir.dt.float4_e2m1fn_x4
-MULT = mybir.AluOpType.mult
 
 P = 128
 PACK = 4
 K_PASS = P * PACK
 PASSES = K // K_PASS
+QUADRANTS, SCALE_ROWS = 4, 4
 TB = 128
 BLOCKS = T // TB
 HALF = T // 2
-SCALAR_COLS = 192
+RUN = 4
+SCALAR_COLS = 160
+W8_PASS, FIRST_PASS, LAST_W4_PASS = 0, 1, PASSES - 1
+LAST = BLOCKS - 1
 
 
 def tile_mix_dyq_fm_pl_mul_kernel(
@@ -48,199 +51,171 @@ def tile_mix_dyq_fm_pl_mul_kernel(
         acc = [ps.tile([P, D], F32, name=f"acc{b}") for b in range(BLOCKS)]
         flip = [ps.tile([P, PACK, TB], F32, name=f"flip{b}") for b in range(BLOCKS)]
         dealt = [sb.tile([P, PACK, P], F32, name=f"dealt{b}", align_bytes=64) for b in range(BLOCKS)]
+        out_f = [sb.tile([P, PACK, TB], F32, name=f"out_f{b}", align_bytes=64) for b in range(BLOCKS)]
         out_bf = [sb.tile([P, TB, PACK], BF16, name=f"out_bf{b}", align_bytes=64) for b in range(BLOCKS)]
+
+        def cols(b):
+            return slice(b * TB, (b + 1) * TB)
 
         def by_partition(rows):
             return rows.rearrange("(p j) w -> p j w", j=PACK)
 
-        def load(src, t0, t1, name):
-            raw = sb.tile([P, PACK, t1 - t0], F32, name=name, align_bytes=64)
-            nc.sync.dma_start(out=raw[:], in_=by_partition(src)[:, :, t0:t1])
-            return raw
+        def load(rows, t0, t1, name):
+            piece = sb.tile([P, PACK, t1 - t0], F32, name=name, align_bytes=64)
+            nc.sync.dma_start(out=piece[:], in_=by_partition(rows)[:, :, t0:t1])
+            return piece
 
-        def dy_rows(a):
-            return dy[a * K_PASS : (a + 1) * K_PASS, :]
+        def load_dy(a, t0, t1):
+            return load(dy[a * K_PASS : (a + 1) * K_PASS, :], t0, t1, f"dy{a}_{t0}")
 
-        nc.vector.memset(w4_sc[:].rearrange("p a n -> p (a n)").bitcast(I32), 0)
-        nc.vector.memset(w8_sc[:].bitcast(I32), 0)
-        make_identity(nc, ident[:])
-
-        def load_w4_scales():
-            for q in range(4):
-                nc.sync.dma_start(
-                    out=w4_sc[q:P:32, :, :].bitcast(I32),
-                    in_=w4_scales[:, q:16:4, :].rearrange("a r n -> r a n").bitcast(I32),
-                )
-
-        def load_w8_scales():
-            for q in range(4):
-                nc.sync.dma_start(
-                    out=w8_sc[q:P:32, :].bitcast(I32),
-                    in_=w8_scales[0, q:16:4, :].bitcast(I32),
-                )
-
-        raw = {}
-        raw[1] = load(dy_rows(1), 0, T, "raw1")
-        load_w4_scales()
-        nc.sync.dma_start(out=w4[:].bitcast(I32), in_=w4_words.rearrange("a p n -> p a n").bitcast(I32))
-        raw[2] = load(dy_rows(2), 0, T, "raw2")
-        third_h0 = load(dy_rows(3), 0, HALF, "third_h0")
-        load_w8_scales()
-        prev_h0 = load(dy_rows(4), 0, HALF, "prev_h0")
-        last_h0 = load(dy_rows(0), 0, HALF, "last_h0")
-        nc.sync.dma_start(out=w8[:].bitcast(I32), in_=w8_words[0].rearrange("p n t -> p (n t)").bitcast(I32))
-        third_h1 = load(dy_rows(3), HALF, T, "third_h1")
-        prev_b2 = load(dy_rows(4), 2 * TB, 3 * TB, "prev_b2")
-        last_b2 = load(dy_rows(0), 2 * TB, 3 * TB, "last_b2")
-        prev_b3 = load(dy_rows(4), 3 * TB, 4 * TB, "prev_b3")
-        last_b3 = load(dy_rows(0), 3 * TB, 4 * TB, "last_b3")
-        g_blk = [load(g, b * TB, (b + 1) * TB, f"g_b{b}")[:] for b in range(BLOCKS)]
-
-        out_f = [sb.tile([P, PACK, TB], F32, name=f"out_b{b}", align_bytes=64)[:] for b in range(BLOCKS)]
-
-        def cast_scalar(dst, src):
-            nc.scalar.copy(
-                out=dst.rearrange("p (c i) j -> p c j i", i=4), in_=src.rearrange("p j (c i) -> p c j i", i=4)
+        def interleave(copy, dst, src):
+            copy(
+                out=dst.rearrange("p (c i) j -> p c j i", i=RUN),
+                in_=src.rearrange("p j (c i) -> p c j i", i=RUN),
             )
 
-        def cast_vector(dst, src):
-            nc.vector.tensor_copy(
-                out=dst.rearrange("p (c i) j -> p c j i", i=4), in_=src.rearrange("p j (c i) -> p c j i", i=4)
-            )
+        on_scalar, on_vector = nc.scalar.copy, nc.vector.tensor_copy
 
-        def quant_dy(a, t0, t1):
+        def quantise_dy(a, span):
             nc.vector.quantize_mx(
-                out=dy_codes[a][:, t0:t1].bitcast(E5M2),
-                scales=dy_sc[a][:, t0:t1],
-                in_=dy_bf[a][:, t0:t1, :].rearrange("p w j -> p (w j)"),
+                out=dy_codes[a][:, span].bitcast(E5M2),
+                scales=dy_sc[a][:, span],
+                in_=dy_bf[a][:, span, :].rearrange("p w j -> p (w j)"),
             )
 
         def product(a, b):
-            cols = slice(b * TB, (b + 1) * TB)
-            if a == 0:
+            if a == W8_PASS:
                 rhs, rhs_scale = w8[:].bitcast(E4M3), w8_sc[:]
             else:
                 rhs, rhs_scale = w4[:, a - 1, :].bitcast(E2M1), w4_sc[:, a - 1, :]
             nc.tensor.matmul_mx(
                 out=acc[b][:],
-                lhsT=dy_codes[a][:, cols].bitcast(E5M2),
-                lhsT_scale=dy_sc[a][:, cols],
+                lhsT=dy_codes[a][:, cols(b)].bitcast(E5M2),
+                lhsT_scale=dy_sc[a][:, cols(b)],
                 rhs=rhs,
                 rhs_scale=rhs_scale,
-                start=(a == 1),
-                stop=(a == 0),
+                start=(a == FIRST_PASS),
+                stop=(a == W8_PASS),
             )
 
-        def deal(b):
-            nc.scalar.copy(out=dealt[b][:], in_=acc[b][:].rearrange("t (m i) -> t i m", i=PACK))
+        def deal(b, slots=slice(0, PACK)):
+            nc.scalar.copy(
+                out=dealt[b][:, slots, :], in_=acc[b][:].rearrange("t (m i) -> t i m", i=PACK)[:, slots, :]
+            )
 
-        def turn(b):
-            for i in range(PACK):
-                nc.tensor.transpose(flip[b][:, i, :], dealt[b][:, i, :], ident[:])
+        def turn(b, bank, slots=slice(0, PACK)):
+            for i in range(slots.start, slots.stop):
+                nc.tensor.transpose(bank[:, i, :], dealt[b][:, i, :], ident[:])
 
-        def gate(b):
-            nc.vector.tensor_tensor(out=out_f[b], in0=flip[b][:], in1=g_blk[b], op=MULT)
+        def gate(b, bank, slots=slice(0, PACK)):
+            nc.vector.tensor_tensor(
+                out=out_f[b][:, slots, :],
+                in0=bank[:, slots, :],
+                in1=g_block[b][:, slots, :],
+                op=mybir.AluOpType.mult,
+            )
 
-        def quant_out(b):
-            cols = slice(b * TB, (b + 1) * TB)
+        def store_out(b):
+            nc.sync.dma_start(out=by_partition(out_0)[:, :, cols(b)], in_=out_f[b][:])
+
+        def quantise_out(b):
             nc.vector.quantize_mx(
-                out=out_codes[:, cols].bitcast(E4M3),
-                scales=out_sc[:, cols],
+                out=out_codes[:, cols(b)].bitcast(E4M3),
+                scales=out_sc[:, cols(b)],
                 in_=out_bf[b][:].rearrange("p w j -> p (w j)"),
             )
 
-        def store_out(src, t0, t1):
-            nc.sync.dma_start(out=by_partition(out_0)[:, :, t0:t1], in_=src)
+        nc.vector.memset(w4_sc[:].rearrange("p a n -> p (a n)").bitcast(I32), 0)
+        nc.vector.memset(w8_sc[:].bitcast(I32), 0)
+        make_identity(nc, ident[:])
 
-        def store_codes(t0, t1):
-            words = out_1[0].rearrange("p t i -> p (t i)").bitcast(I32)
-            nc.sync.dma_start(out=words[:, t0:t1], in_=out_codes[:, t0:t1].bitcast(I32))
+        dy_whole = {FIRST_PASS: load_dy(FIRST_PASS, 0, T)}
+        for r in range(SCALE_ROWS):
+            nc.sync.dma_start(
+                out=w4_sc[r:P:32, :, :].bitcast(I32),
+                in_=w4_scales[:, r:16:SCALE_ROWS, :].rearrange("a q n -> q a n").bitcast(I32),
+            )
+        nc.sync.dma_start(out=w4[:].bitcast(I32), in_=w4_words.rearrange("a p n -> p a n").bitcast(I32))
+        for a in range(FIRST_PASS + 1, LAST_W4_PASS):
+            dy_whole[a] = load_dy(a, 0, T)
+        for r in range(SCALE_ROWS):
+            nc.sync.dma_start(
+                out=w8_sc[r:P:32, :].bitcast(I32), in_=w8_scales[0, r:16:SCALE_ROWS, :].bitcast(I32)
+            )
+        dy_whole[LAST_W4_PASS] = load_dy(LAST_W4_PASS, 0, T)
+        dy_front = load_dy(W8_PASS, 0, HALF)
+        nc.sync.dma_start(out=w8[:].bitcast(I32), in_=w8_words[0].rearrange("p n j -> p (n j)").bitcast(I32))
+        dy_w8 = [dy_front[:, :, cols(0)], dy_front[:, :, cols(1)]]
+        dy_w8 += [load_dy(W8_PASS, b * TB, (b + 1) * TB)[:] for b in (2, LAST)]
+        g_half = [load(g, h * HALF, (h + 1) * HALF, f"g{h}") for h in range(2)]
+        g_block = [g_half[b // 2][:, :, cols(b % 2)] for b in range(BLOCKS)]
 
-        def blk(a, b):
-            return dy_bf[a][:, b * TB : (b + 1) * TB, :]
-
-        def quant_blk(a, b):
-            quant_dy(a, b * TB, (b + 1) * TB)
-
-        spare = acc[0][:].rearrange("p (i t) -> p i t", i=PACK)
-        banks3 = (flip[3][:], spare)
-
-        def deal_turn_last():
-            for u in range(2):
-                nc.scalar.copy(
-                    out=dealt[3][:, 2 * u : 2 * u + 2, :],
-                    in_=acc[3][:].rearrange("t (m i) -> t i m", i=PACK)[:, 2 * u : 2 * u + 2, :],
-                )
-                for i in (2 * u, 2 * u + 1):
-                    nc.tensor.transpose(banks3[u][:, i, :], dealt[3][:, i, :], ident[:])
-
-        def gate_last():
-            for u in range(2):
-                nc.vector.tensor_tensor(
-                    out=out_f[3][:, 2 * u : 2 * u + 2, :],
-                    in0=banks3[u][:, 2 * u : 2 * u + 2, :],
-                    in1=g_blk[3][:, 2 * u : 2 * u + 2, :],
-                    op=MULT,
-                )
-
-        for a in range(1, PASSES - 2):
-            cast_scalar(dy_bf[a][:, 0:SCALAR_COLS, :], raw[a][:, :, 0:SCALAR_COLS])
-            cast_vector(dy_bf[a][:, SCALAR_COLS:T, :], raw[a][:, :, SCALAR_COLS:T])
-            quant_dy(a, 0, T)
+        for a in range(FIRST_PASS, LAST_W4_PASS):
+            interleave(on_scalar, dy_bf[a][:, :SCALAR_COLS, :], dy_whole[a][:, :, :SCALAR_COLS])
+            interleave(on_vector, dy_bf[a][:, SCALAR_COLS:, :], dy_whole[a][:, :, SCALAR_COLS:])
+            quantise_dy(a, slice(0, T))
             for b in range(BLOCKS):
                 product(a, b)
 
-        for a, src in ((3, third_h0), (4, prev_h0), (0, last_h0)):
-            cast_scalar(blk(a, 0), src[:, :, 0:TB])
-            cast_vector(blk(a, 1), src[:, :, TB:HALF])
-            quant_blk(a, 0)
-            quant_blk(a, 1)
-            product(a, 0)
-            product(a, 1)
-        deal(0)
-        deal(1)
-        turn(0)
-        cast_vector(dy_bf[3][:, HALF:T, :], third_h1[:])
-        cast_vector(blk(4, 2), prev_b2[:])
-        quant_dy(3, HALF, T)
-        cast_vector(blk(0, 2), last_b2[:])
-        quant_blk(4, 2)
-        cast_scalar(blk(4, 3), prev_b3[:])
-        quant_blk(0, 2)
-        turn(1)
-        product(3, 2)
-        product(4, 2)
-        product(0, 2)
-        product(3, 3)
+        def round_w4(copy, b):
+            interleave(copy, dy_bf[LAST_W4_PASS][:, cols(b), :], dy_whole[LAST_W4_PASS][:, :, cols(b)])
+
+        def round_w8(copy, b):
+            interleave(copy, dy_bf[W8_PASS][:, cols(b), :], dy_w8[b])
+
+        round_w4(on_scalar, 2)
+        round_w4(on_scalar, 3)
+        round_w4(on_vector, 0)
+        round_w4(on_vector, 1)
+        for b in range(LAST):
+            quantise_dy(LAST_W4_PASS, cols(b))
+            product(LAST_W4_PASS, b)
+        round_w8(on_vector, 0)
+        round_w8(on_scalar, 1)
+        quantise_dy(LAST_W4_PASS, cols(LAST))
+        product(LAST_W4_PASS, LAST)
+        for b in (0, 1):
+            quantise_dy(W8_PASS, cols(b))
+            product(W8_PASS, b)
+            deal(b)
+        for b in (2, LAST):
+            round_w8(on_vector, b)
+            quantise_dy(W8_PASS, cols(b))
+
+        product(W8_PASS, 2)
+        turn(0, flip[0])
+        product(W8_PASS, LAST)
         deal(2)
-        cast_vector(blk(0, 3), last_b3[:])
-        quant_blk(4, 3)
-        quant_blk(0, 3)
-        product(4, 3)
-        product(0, 3)
-        turn(2)
-        gate(0)
-        store_out(out_f[0], 0, TB)
-        deal_turn_last()
-        cast_scalar(out_bf[0][:], out_f[0])
-        gate(1)
-        store_out(out_f[1], TB, HALF)
-        cast_scalar(out_bf[1][:], out_f[1])
-        gate(2)
-        store_out(out_f[2], 2 * TB, 3 * TB)
-        cast_scalar(out_bf[2][:], out_f[2])
-        gate_last()
-        store_out(out_f[3], 3 * TB, 4 * TB)
-        quant_out(0)
-        cast_vector(out_bf[3][:], out_f[3])
-        quant_out(1)
-        store_codes(0, HALF)
-        quant_out(2)
-        quant_out(3)
-        store_codes(HALF, T)
-        for q in range(4):
-            eng = nc.scalar if q % 2 == 0 else nc.sync
-            eng.dma_start(
-                out=out_2[0, 4 * q : 4 * q + 4, :].bitcast(I32),
-                in_=out_sc[32 * q : 32 * q + 4, :].bitcast(I32),
+        turn(1, flip[1])
+        turn(2, flip[2])
+
+        halves = (
+            (flip[LAST], slice(0, 2)),
+            (acc[0][:].rearrange("p (i t) -> p i t", i=PACK), slice(2, PACK)),
+        )
+        for bank, slots in halves:
+            deal(LAST, slots)
+            turn(LAST, bank, slots)
+
+        for b in range(LAST):
+            gate(b, flip[b])
+            store_out(b)
+            interleave(on_scalar, out_bf[b][:], out_f[b][:])
+        for bank, slots in halves:
+            gate(LAST, bank, slots)
+        store_out(LAST)
+
+        quantise_out(0)
+        quantise_out(1)
+        interleave(on_vector, out_bf[LAST][:], out_f[LAST][:])
+        quantise_out(2)
+        quantise_out(LAST)
+        nc.sync.dma_start(
+            out=out_1[0].rearrange("p t i -> p (t i)").bitcast(I32), in_=out_codes[:].bitcast(I32)
+        )
+        for q in range(QUADRANTS):
+            queue = nc.scalar if q % 2 == 0 else nc.sync
+            queue.dma_start(
+                out=out_2[0, SCALE_ROWS * q : SCALE_ROWS * (q + 1), :].bitcast(I32),
+                in_=out_sc[32 * q : 32 * q + SCALE_ROWS, :].bitcast(I32),
             )

@@ -1,7 +1,6 @@
 from contextlib import ExitStack
 
 import concourse.mybir as mybir
-from concourse.masks import make_identity
 
 K, D, T = 2560, 512, 512
 FLOPS = 2 * K * D * T
@@ -10,6 +9,7 @@ F32 = mybir.dt.float32
 BF16 = mybir.dt.bfloat16
 I32 = mybir.dt.int32
 U32 = mybir.dt.uint32
+U16 = mybir.dt.uint16
 U8 = mybir.dt.uint8
 E4M3 = mybir.dt.float8_e4m3fn_x4
 E5M2 = mybir.dt.float8_e5m2_x4
@@ -19,14 +19,14 @@ P = 128
 PACK = 4
 K_PASS = P * PACK
 PASSES = K // K_PASS
+W4_PASSES = PASSES - 1
 QUADRANTS, SCALE_ROWS = 4, 4
-TB = 128
-BLOCKS = T // TB
+QUARTER = T // 4
 HALF = T // 2
 RUN = 4
-SCALAR_COLS = 160
 W8_PASS, FIRST_PASS, LAST_W4_PASS = 0, 1, PASSES - 1
-LAST = BLOCKS - 1
+SCALAR_COLS = 320
+OUT_SCALAR_COLS = 64
 
 
 def tile_mix_dyq_fm_pl_mul_kernel(
@@ -38,35 +38,33 @@ def tile_mix_dyq_fm_pl_mul_kernel(
         ps = ctx.enter_context(tc.psum_pool(name="ps", bufs=1))
         ctx.enter_context(tc.manual_schedule())
 
-        w8 = sb.tile([P, D], U32, name="w8", align_bytes=64)
-        w4 = sb.tile([P, PASSES - 1, 2 * D], U8, name="w4", align_bytes=64)
-        w4_sc = sb.tile([P, PASSES - 1, D], U8, name="w4_sc", align_bytes=64)
+        w8_raw = sb.tile([P, D], I32, name="w8_raw", align_bytes=64)
+        w4_raw = sb.tile([P, W4_PASSES, 2 * D], U8, name="w4_raw", align_bytes=64)
+        w4_sc_raw = sb.tile([P, W4_PASSES, D], U8, name="w4_sc_raw", align_bytes=64)
+        w8_sc_raw = sb.tile([P, D], U8, name="w8_sc_raw", align_bytes=64)
+        w8_first = sb.tile([P, 1, P], I32, name="w8_first", align_bytes=64)
+        w8_rest = sb.tile([P, PACK - 1, P], I32, name="w8_rest", align_bytes=64)
+        w8 = [w8_first[:, 0, :]] + [w8_rest[:, i, :] for i in range(PACK - 1)]
         w8_sc = sb.tile([P, D], U8, name="w8_sc", align_bytes=64)
-        ident = sb.tile([P, P], F32, name="ident", align_bytes=64)
+        w4 = sb.tile([P, W4_PASSES, 2 * D], U8, name="w4", align_bytes=64)
+        w4_sc = sb.tile([P, W4_PASSES, D], U8, name="w4_sc", align_bytes=64)
         dy_codes = [sb.tile([P, T], U32, name=f"dy_codes{a}", align_bytes=64) for a in range(PASSES)]
         dy_sc = [sb.tile([P, T], U8, name=f"dy_sc{a}", align_bytes=64) for a in range(PASSES)]
         dy_bf = [sb.tile([P, T, PACK], BF16, name=f"dy_bf{a}", align_bytes=64) for a in range(PASSES)]
         out_codes = sb.tile([P, T], U32, name="out_codes", align_bytes=64)
         out_sc = sb.tile([P, T], U8, name="out_sc", align_bytes=64)
-        acc = [ps.tile([P, D], F32, name=f"acc{b}") for b in range(BLOCKS)]
-        flip = [ps.tile([P, PACK, TB], F32, name=f"flip{b}") for b in range(BLOCKS)]
-        dealt = [sb.tile([P, PACK, P], F32, name=f"dealt{b}", align_bytes=64) for b in range(BLOCKS)]
-        out_f = [sb.tile([P, PACK, TB], F32, name=f"out_f{b}", align_bytes=64) for b in range(BLOCKS)]
-        out_bf = [sb.tile([P, TB, PACK], BF16, name=f"out_bf{b}", align_bytes=64) for b in range(BLOCKS)]
-
-        def cols(b):
-            return slice(b * TB, (b + 1) * TB)
+        out_f = sb.tile([P, PACK, T], F32, name="out_f", align_bytes=64)
+        out_bf = sb.tile([P, T, PACK], BF16, name="out_bf", align_bytes=64)
+        acc = [ps.tile([P, T], F32, name=f"acc{i}") for i in range(PACK)]
 
         def by_partition(rows):
             return rows.rearrange("(p j) w -> p j w", j=PACK)
 
-        def load(rows, t0, t1, name):
-            piece = sb.tile([P, PACK, t1 - t0], F32, name=name, align_bytes=64)
+        def load_dy(a, t0, t1):
+            piece = sb.tile([P, PACK, t1 - t0], F32, name=f"dy{a}_{t0}", align_bytes=64)
+            rows = dy[a * K_PASS : (a + 1) * K_PASS, :]
             nc.sync.dma_start(out=piece[:], in_=by_partition(rows)[:, :, t0:t1])
             return piece
-
-        def load_dy(a, t0, t1):
-            return load(dy[a * K_PASS : (a + 1) * K_PASS, :], t0, t1, f"dy{a}_{t0}")
 
         def interleave(copy, dst, src):
             copy(
@@ -76,143 +74,144 @@ def tile_mix_dyq_fm_pl_mul_kernel(
 
         on_scalar, on_vector = nc.scalar.copy, nc.vector.tensor_copy
 
-        def quantise_dy(a, span):
+        def deal(dst, src, run):
+            nc.vector.tensor_copy(
+                out=dst.rearrange("p a (i c m) -> p a c i m", i=PACK, m=run),
+                in_=src.rearrange("p a (c m i) -> p a c i m", i=PACK, m=run),
+            )
+
+        def quantise_dy(a, t0, t1):
             nc.vector.quantize_mx(
-                out=dy_codes[a][:, span].bitcast(E5M2),
-                scales=dy_sc[a][:, span],
-                in_=dy_bf[a][:, span, :].rearrange("p w j -> p (w j)"),
+                out=dy_codes[a][:, t0:t1].bitcast(E5M2),
+                scales=dy_sc[a][:, t0:t1],
+                in_=dy_bf[a][:, t0:t1, :].rearrange("p w j -> p (w j)"),
             )
 
-        def product(a, b):
-            if a == W8_PASS:
-                rhs, rhs_scale = w8[:].bitcast(E4M3), w8_sc[:]
-            else:
-                rhs, rhs_scale = w4[:, a - 1, :].bitcast(E2M1), w4_sc[:, a - 1, :]
-            nc.tensor.matmul_mx(
-                out=acc[b][:],
-                lhsT=dy_codes[a][:, cols(b)].bitcast(E5M2),
-                lhsT_scale=dy_sc[a][:, cols(b)],
-                rhs=rhs,
-                rhs_scale=rhs_scale,
-                start=(a == FIRST_PASS),
-                stop=(a == W8_PASS),
+        def deal_w8(dst, i0, i1):
+            nc.vector.tensor_copy(
+                out=dst[:].rearrange("p i (c m) -> p c i m", m=RUN),
+                in_=w8_raw[:].rearrange("p (c m i) -> p c i m", i=PACK, m=RUN)[:, :, i0:i1, :],
             )
 
-        def deal(b, slots=slice(0, PACK)):
-            nc.scalar.copy(
-                out=dealt[b][:, slots, :], in_=acc[b][:].rearrange("t (m i) -> t i m", i=PACK)[:, slots, :]
-            )
+        def products(a, slots=range(PACK)):
+            for i in slots:
+                m = slice(i * P, (i + 1) * P)
+                if a == W8_PASS:
+                    lhsT, lhsT_scale = w8[i].bitcast(E4M3), w8_sc[:, m]
+                else:
+                    lhsT = w4[:, a - 1, 2 * i * P : 2 * (i + 1) * P].bitcast(E2M1)
+                    lhsT_scale = w4_sc[:, a - 1, m]
+                nc.tensor.matmul_mx(
+                    out=acc[i][:],
+                    lhsT=lhsT,
+                    lhsT_scale=lhsT_scale,
+                    rhs=dy_codes[a][:].bitcast(E5M2),
+                    rhs_scale=dy_sc[a][:],
+                    start=(a == FIRST_PASS),
+                    stop=(a == W8_PASS),
+                )
 
-        def turn(b, bank, slots=slice(0, PACK)):
-            for i in range(slots.start, slots.stop):
-                nc.tensor.transpose(bank[:, i, :], dealt[b][:, i, :], ident[:])
-
-        def gate(b, bank, slots=slice(0, PACK)):
+        def gate(i, t0, t1):
             nc.vector.tensor_tensor(
-                out=out_f[b][:, slots, :],
-                in0=bank[:, slots, :],
-                in1=g_block[b][:, slots, :],
+                out=out_f[:, i, t0:t1],
+                in0=acc[i][:, t0:t1],
+                in1=g_pair[i // 2][:, i % 2, t0:t1],
                 op=mybir.AluOpType.mult,
             )
 
-        def store_out(b):
-            nc.sync.dma_start(out=by_partition(out_0)[:, :, cols(b)], in_=out_f[b][:])
+        def store_out(i):
+            nc.sync.dma_start(out=by_partition(out_0)[:, i, :], in_=out_f[:, i, :])
 
-        def quantise_out(b):
+        def quantise_out(t0, t1):
             nc.vector.quantize_mx(
-                out=out_codes[:, cols(b)].bitcast(E4M3),
-                scales=out_sc[:, cols(b)],
-                in_=out_bf[b][:].rearrange("p w j -> p (w j)"),
+                out=out_codes[:, t0:t1].bitcast(E4M3),
+                scales=out_sc[:, t0:t1],
+                in_=out_bf[:, t0:t1, :].rearrange("p w j -> p (w j)"),
             )
 
-        nc.vector.memset(w4_sc[:].rearrange("p a n -> p (a n)").bitcast(I32), 0)
-        nc.vector.memset(w8_sc[:].bitcast(I32), 0)
-        make_identity(nc, ident[:])
+        def store_codes(t0, t1):
+            nc.sync.dma_start(
+                out=out_1[0].rearrange("p t i -> p (t i)").bitcast(I32)[:, t0:t1],
+                in_=out_codes[:, t0:t1].bitcast(I32),
+            )
 
-        dy_whole = {FIRST_PASS: load_dy(FIRST_PASS, 0, T)}
+        nc.vector.memset(w4_sc_raw[:].rearrange("p a n -> p (a n)").bitcast(I32), 0)
+        nc.vector.memset(w8_sc_raw[:].bitcast(I32), 0)
+
+        nc.sync.dma_start(
+            out=w4_raw[:].bitcast(I32), in_=w4_words.rearrange("a p n -> p a n").bitcast(I32)
+        )
         for r in range(SCALE_ROWS):
             nc.sync.dma_start(
-                out=w4_sc[r:P:32, :, :].bitcast(I32),
+                out=w4_sc_raw[r:P:32, :, :].bitcast(I32),
                 in_=w4_scales[:, r:16:SCALE_ROWS, :].rearrange("a q n -> q a n").bitcast(I32),
             )
-        nc.sync.dma_start(out=w4[:].bitcast(I32), in_=w4_words.rearrange("a p n -> p a n").bitcast(I32))
-        for a in range(FIRST_PASS + 1, LAST_W4_PASS):
-            dy_whole[a] = load_dy(a, 0, T)
+        dy_whole = {FIRST_PASS: load_dy(FIRST_PASS, 0, T)}
+        dy_whole[2] = load_dy(2, 0, T)
         for r in range(SCALE_ROWS):
             nc.sync.dma_start(
-                out=w8_sc[r:P:32, :].bitcast(I32), in_=w8_scales[0, r:16:SCALE_ROWS, :].bitcast(I32)
+                out=w8_sc_raw[r:P:32, :].bitcast(I32), in_=w8_scales[0, r:16:SCALE_ROWS, :].bitcast(I32)
             )
-        dy_whole[LAST_W4_PASS] = load_dy(LAST_W4_PASS, 0, T)
-        dy_front = load_dy(W8_PASS, 0, HALF)
-        nc.sync.dma_start(out=w8[:].bitcast(I32), in_=w8_words[0].rearrange("p n j -> p (n j)").bitcast(I32))
-        dy_w8 = [dy_front[:, :, cols(0)], dy_front[:, :, cols(1)]]
-        dy_w8 += [load_dy(W8_PASS, b * TB, (b + 1) * TB)[:] for b in (2, LAST)]
-        g_half = [load(g, h * HALF, (h + 1) * HALF, f"g{h}") for h in range(2)]
-        g_block = [g_half[b // 2][:, :, cols(b % 2)] for b in range(BLOCKS)]
+        for a in range(3, PASSES):
+            dy_whole[a] = load_dy(a, 0, T)
+        front = load_dy(W8_PASS, 0, T - QUARTER)
+        back = load_dy(W8_PASS, T - QUARTER, T)
+        nc.sync.dma_start(out=w8_raw[:], in_=w8_words[0].rearrange("p n j -> p (n j)").bitcast(I32))
+        g_pair = []
+        for h in range(2):
+            pair = sb.tile([P, 2, T], F32, name=f"g{h}", align_bytes=64)
+            nc.sync.dma_start(out=pair[:], in_=by_partition(g)[:, 2 * h : 2 * h + 2, :])
+            g_pair.append(pair)
+
+        deal(w4[:].bitcast(U16), w4_raw[:].bitcast(U16), 8)
+        deal(w4_sc[:], w4_sc_raw[:], 16)
 
         for a in range(FIRST_PASS, LAST_W4_PASS):
-            interleave(on_scalar, dy_bf[a][:, :SCALAR_COLS, :], dy_whole[a][:, :, :SCALAR_COLS])
-            interleave(on_vector, dy_bf[a][:, SCALAR_COLS:, :], dy_whole[a][:, :, SCALAR_COLS:])
-            quantise_dy(a, slice(0, T))
-            for b in range(BLOCKS):
-                product(a, b)
+            src = dy_whole[a]
+            interleave(on_scalar, dy_bf[a][:, :SCALAR_COLS, :], src[:, :, :SCALAR_COLS])
+            interleave(on_vector, dy_bf[a][:, SCALAR_COLS:, :], src[:, :, SCALAR_COLS:])
+            if a == 2:
+                deal(w8_sc[:].unsqueeze(1), w8_sc_raw[:].unsqueeze(1), 16)
+            quantise_dy(a, 0, T)
+            products(a)
 
-        def round_w4(copy, b):
-            interleave(copy, dy_bf[LAST_W4_PASS][:, cols(b), :], dy_whole[LAST_W4_PASS][:, :, cols(b)])
+        a = LAST_W4_PASS
+        src = dy_whole[a]
+        interleave(on_scalar, dy_bf[a][:, :QUARTER, :], src[:, :, :QUARTER])
+        interleave(on_scalar, dy_bf[a][:, QUARTER:HALF, :], src[:, :, QUARTER:HALF])
+        interleave(on_vector, dy_bf[a][:, HALF:, :], src[:, :, HALF:])
+        quantise_dy(a, 0, QUARTER)
+        quantise_dy(a, HALF, T)
+        quantise_dy(a, QUARTER, HALF)
+        products(a)
 
-        def round_w8(copy, b):
-            interleave(copy, dy_bf[W8_PASS][:, cols(b), :], dy_w8[b])
+        a = W8_PASS
+        interleave(on_scalar, dy_bf[a][:, HALF : T - QUARTER, :], front[:, :, HALF:])
+        interleave(on_scalar, dy_bf[a][:, T - QUARTER :, :], back[:])
+        interleave(on_vector, dy_bf[a][:, :HALF, :], front[:, :, :HALF])
+        quantise_dy(a, HALF, T - QUARTER)
+        quantise_dy(a, 0, HALF)
+        deal_w8(w8_first, 0, 1)
+        quantise_dy(a, T - QUARTER, T)
+        products(a, range(1))
+        deal_w8(w8_rest, 1, PACK)
+        products(a, range(1, PACK))
 
-        round_w4(on_scalar, 2)
-        round_w4(on_scalar, 3)
-        round_w4(on_vector, 0)
-        round_w4(on_vector, 1)
-        for b in range(LAST):
-            quantise_dy(LAST_W4_PASS, cols(b))
-            product(LAST_W4_PASS, b)
-        round_w8(on_vector, 0)
-        round_w8(on_scalar, 1)
-        quantise_dy(LAST_W4_PASS, cols(LAST))
-        product(LAST_W4_PASS, LAST)
-        for b in (0, 1):
-            quantise_dy(W8_PASS, cols(b))
-            product(W8_PASS, b)
-            deal(b)
-        for b in (2, LAST):
-            round_w8(on_vector, b)
-            quantise_dy(W8_PASS, cols(b))
-
-        product(W8_PASS, 2)
-        turn(0, flip[0])
-        product(W8_PASS, LAST)
-        deal(2)
-        turn(1, flip[1])
-        turn(2, flip[2])
-
-        halves = (
-            (flip[LAST], slice(0, 2)),
-            (acc[0][:].rearrange("p (i t) -> p i t", i=PACK), slice(2, PACK)),
-        )
-        for bank, slots in halves:
-            deal(LAST, slots)
-            turn(LAST, bank, slots)
-
-        for b in range(LAST):
-            gate(b, flip[b])
-            store_out(b)
-            interleave(on_scalar, out_bf[b][:], out_f[b][:])
-        for bank, slots in halves:
-            gate(LAST, bank, slots)
-        store_out(LAST)
-
-        quantise_out(0)
-        quantise_out(1)
-        interleave(on_vector, out_bf[LAST][:], out_f[LAST][:])
-        quantise_out(2)
-        quantise_out(LAST)
-        nc.sync.dma_start(
-            out=out_1[0].rearrange("p t i -> p (t i)").bitcast(I32), in_=out_codes[:].bitcast(I32)
-        )
+        gate(0, 0, T)
+        store_out(0)
+        for i in range(1, PACK):
+            gate(i, 0, HALF)
+        interleave(on_scalar, out_bf[:, :HALF, :], out_f[:, :, :HALF])
+        for i in range(1, PACK):
+            gate(i, HALF, T)
+            store_out(i)
+        cut = HALF + OUT_SCALAR_COLS
+        interleave(on_scalar, out_bf[:, HALF:cut, :], out_f[:, :, HALF:cut])
+        interleave(on_vector, out_bf[:, cut:, :], out_f[:, :, cut:])
+        quantise_out(0, HALF)
+        store_codes(0, HALF)
+        quantise_out(HALF, T)
+        store_codes(HALF, T)
         for q in range(QUADRANTS):
             queue = nc.scalar if q % 2 == 0 else nc.sync
             queue.dma_start(

@@ -119,8 +119,8 @@ def tile_mix_dyq_fm_pl_mul_kernel(
                 op=mybir.AluOpType.mult,
             )
 
-        def store_out(i):
-            nc.sync.dma_start(out=by_partition(out_0)[:, i, :], in_=out_f[:, i, :])
+        def store_out(i0, i1):
+            nc.sync.dma_start(out=by_partition(out_0)[:, i0:i1, :], in_=out_f[:, i0:i1, :])
 
         def quantise_out(t0, t1):
             nc.vector.quantize_mx(
@@ -141,12 +141,12 @@ def tile_mix_dyq_fm_pl_mul_kernel(
         nc.sync.dma_start(
             out=w4_raw[:].bitcast(I32), in_=w4_words.rearrange("a p n -> p a n").bitcast(I32)
         )
+        dy_whole = {FIRST_PASS: load_dy(FIRST_PASS, 0, T)}
         for r in range(SCALE_ROWS):
             nc.sync.dma_start(
                 out=w4_sc_raw[r:P:32, :, :].bitcast(I32),
                 in_=w4_scales[:, r:16:SCALE_ROWS, :].rearrange("a q n -> q a n").bitcast(I32),
             )
-        dy_whole = {FIRST_PASS: load_dy(FIRST_PASS, 0, T)}
         dy_whole[2] = load_dy(2, 0, T)
         for r in range(SCALE_ROWS):
             nc.sync.dma_start(
@@ -164,12 +164,13 @@ def tile_mix_dyq_fm_pl_mul_kernel(
             g_pair.append(pair)
 
         deal(w4[:].bitcast(U16), w4_raw[:].bitcast(U16), 8)
-        deal(w4_sc[:], w4_sc_raw[:], 16)
 
         for a in range(FIRST_PASS, LAST_W4_PASS):
             src = dy_whole[a]
             interleave(on_scalar, dy_bf[a][:, :SCALAR_COLS, :], src[:, :, :SCALAR_COLS])
             interleave(on_vector, dy_bf[a][:, SCALAR_COLS:, :], src[:, :, SCALAR_COLS:])
+            if a == FIRST_PASS:
+                deal(w4_sc[:], w4_sc_raw[:], 16)
             if a == 2:
                 deal(w8_sc[:].unsqueeze(1), w8_sc_raw[:].unsqueeze(1), 16)
             quantise_dy(a, 0, T)
@@ -198,13 +199,15 @@ def tile_mix_dyq_fm_pl_mul_kernel(
         products(a, range(1, PACK))
 
         gate(0, 0, T)
-        store_out(0)
+        store_out(0, 1)
         for i in range(1, PACK):
             gate(i, 0, HALF)
         interleave(on_scalar, out_bf[:, :HALF, :], out_f[:, :, :HALF])
-        for i in range(1, PACK):
+        gate(1, HALF, T)
+        store_out(1, 2)
+        for i in range(2, PACK):
             gate(i, HALF, T)
-            store_out(i)
+        store_out(2, PACK)
         cut = HALF + OUT_SCALAR_COLS
         interleave(on_scalar, out_bf[:, HALF:cut, :], out_f[:, :, HALF:cut])
         interleave(on_vector, out_bf[:, cut:, :], out_f[:, :, cut:])

@@ -26,7 +26,6 @@ HALF = T // 2
 RUN = 4
 W8_PASS, FIRST_PASS, LAST_W4_PASS = 0, 1, PASSES - 1
 SCALAR_COLS = 320
-OUT_SCALAR_COLS = 64
 
 
 def tile_mix_dyq_fm_pl_mul_kernel(
@@ -55,6 +54,7 @@ def tile_mix_dyq_fm_pl_mul_kernel(
         out_sc = sb.tile([P, T], U8, name="out_sc", align_bytes=64)
         out_f = sb.tile([P, PACK, T], F32, name="out_f", align_bytes=64)
         out_bf = sb.tile([P, T, PACK], BF16, name="out_bf", align_bytes=64)
+        sum_1 = sb.tile([P, T], F32, name="sum_1", align_bytes=64)
         acc = [ps.tile([P, T], F32, name=f"acc{i}") for i in range(PACK)]
 
         def by_partition(rows):
@@ -115,12 +115,12 @@ def tile_mix_dyq_fm_pl_mul_kernel(
             nc.vector.tensor_tensor(
                 out=out_f[:, i, t0:t1],
                 in0=acc[i][:, t0:t1],
-                in1=g_pair[i // 2][:, i % 2, t0:t1],
+                in1=g_slot[i][:, t0:t1],
                 op=mybir.AluOpType.mult,
             )
 
-        def store_out(i0, i1):
-            nc.sync.dma_start(out=by_partition(out_0)[:, i0:i1, :], in_=out_f[:, i0:i1, :])
+        def store_out(i0, i1, t0, t1):
+            nc.sync.dma_start(out=by_partition(out_0)[:, i0:i1, t0:t1], in_=out_f[:, i0:i1, t0:t1])
 
         def quantise_out(t0, t1):
             nc.vector.quantize_mx(
@@ -141,12 +141,12 @@ def tile_mix_dyq_fm_pl_mul_kernel(
         nc.sync.dma_start(
             out=w4_raw[:].bitcast(I32), in_=w4_words.rearrange("a p n -> p a n").bitcast(I32)
         )
-        dy_whole = {FIRST_PASS: load_dy(FIRST_PASS, 0, T)}
         for r in range(SCALE_ROWS):
             nc.sync.dma_start(
                 out=w4_sc_raw[r:P:32, :, :].bitcast(I32),
                 in_=w4_scales[:, r:16:SCALE_ROWS, :].rearrange("a q n -> q a n").bitcast(I32),
             )
+        dy_whole = {FIRST_PASS: load_dy(FIRST_PASS, 0, T)}
         dy_whole[2] = load_dy(2, 0, T)
         for r in range(SCALE_ROWS):
             nc.sync.dma_start(
@@ -157,20 +157,19 @@ def tile_mix_dyq_fm_pl_mul_kernel(
         front = load_dy(W8_PASS, 0, T - QUARTER)
         back = load_dy(W8_PASS, T - QUARTER, T)
         nc.sync.dma_start(out=w8_raw[:], in_=w8_words[0].rearrange("p n j -> p (n j)").bitcast(I32))
-        g_pair = []
-        for h in range(2):
-            pair = sb.tile([P, 2, T], F32, name=f"g{h}", align_bytes=64)
-            nc.sync.dma_start(out=pair[:], in_=by_partition(g)[:, 2 * h : 2 * h + 2, :])
-            g_pair.append(pair)
+        g_slot = []
+        for i0, i1 in ((0, 2), (2, 3), (3, PACK)):
+            piece = sb.tile([P, i1 - i0, T], F32, name=f"g{i0}", align_bytes=64)
+            nc.sync.dma_start(out=piece[:], in_=by_partition(g)[:, i0:i1, :])
+            g_slot.extend(piece[:, i, :] for i in range(i1 - i0))
 
         deal(w4[:].bitcast(U16), w4_raw[:].bitcast(U16), 8)
+        deal(w4_sc[:], w4_sc_raw[:], 16)
 
         for a in range(FIRST_PASS, LAST_W4_PASS):
             src = dy_whole[a]
             interleave(on_scalar, dy_bf[a][:, :SCALAR_COLS, :], src[:, :, :SCALAR_COLS])
             interleave(on_vector, dy_bf[a][:, SCALAR_COLS:, :], src[:, :, SCALAR_COLS:])
-            if a == FIRST_PASS:
-                deal(w4_sc[:], w4_sc_raw[:], 16)
             if a == 2:
                 deal(w8_sc[:].unsqueeze(1), w8_sc_raw[:].unsqueeze(1), 16)
             quantise_dy(a, 0, T)
@@ -199,18 +198,20 @@ def tile_mix_dyq_fm_pl_mul_kernel(
         products(a, range(1, PACK))
 
         gate(0, 0, T)
-        store_out(0, 1)
-        for i in range(1, PACK):
+        store_out(0, 1, 0, T)
+        for h in (slice(0, HALF), slice(HALF, T)):
+            on_scalar(out=sum_1[:, h], in_=acc[1][:, h])
+            nc.gpsimd.tensor_tensor(
+                out=out_f[:, 1, h], in0=sum_1[:, h], in1=g_slot[1][:, h], op=mybir.AluOpType.mult
+            )
+        for i in range(2, PACK):
             gate(i, 0, HALF)
+        store_out(1, PACK, 0, HALF)
         interleave(on_scalar, out_bf[:, :HALF, :], out_f[:, :, :HALF])
-        gate(1, HALF, T)
-        store_out(1, 2)
         for i in range(2, PACK):
             gate(i, HALF, T)
-        store_out(2, PACK)
-        cut = HALF + OUT_SCALAR_COLS
-        interleave(on_scalar, out_bf[:, HALF:cut, :], out_f[:, :, HALF:cut])
-        interleave(on_vector, out_bf[:, cut:, :], out_f[:, :, cut:])
+        store_out(1, PACK, HALF, T)
+        interleave(on_vector, out_bf[:, HALF:, :], out_f[:, :, HALF:])
         quantise_out(0, HALF)
         store_codes(0, HALF)
         quantise_out(HALF, T)

@@ -25,7 +25,6 @@ QUARTER = T // 4
 HALF = T // 2
 RUN = 4
 W8_PASS, FIRST_PASS, LAST_W4_PASS = 0, 1, PASSES - 1
-SCALAR_COLS = 320
 
 
 def tile_mix_dyq_fm_pl_mul_kernel(
@@ -54,7 +53,6 @@ def tile_mix_dyq_fm_pl_mul_kernel(
         out_sc = sb.tile([P, T], U8, name="out_sc", align_bytes=64)
         out_f = sb.tile([P, PACK, T], F32, name="out_f", align_bytes=64)
         out_bf = sb.tile([P, T, PACK], BF16, name="out_bf", align_bytes=64)
-        sum_1 = sb.tile([P, T], F32, name="sum_1", align_bytes=64)
         acc = [ps.tile([P, T], F32, name=f"acc{i}") for i in range(PACK)]
 
         def by_partition(rows):
@@ -115,7 +113,7 @@ def tile_mix_dyq_fm_pl_mul_kernel(
             nc.vector.tensor_tensor(
                 out=out_f[:, i, t0:t1],
                 in0=acc[i][:, t0:t1],
-                in1=g_slot[i][:, t0:t1],
+                in1=g_at(i, t0, t1),
                 op=mybir.AluOpType.mult,
             )
 
@@ -157,19 +155,26 @@ def tile_mix_dyq_fm_pl_mul_kernel(
         front = load_dy(W8_PASS, 0, T - QUARTER)
         back = load_dy(W8_PASS, T - QUARTER, T)
         nc.sync.dma_start(out=w8_raw[:], in_=w8_words[0].rearrange("p n j -> p (n j)").bitcast(I32))
-        g_slot = []
-        for i0, i1 in ((0, 2), (2, 3), (3, PACK)):
-            piece = sb.tile([P, i1 - i0, T], F32, name=f"g{i0}", align_bytes=64)
-            nc.sync.dma_start(out=piece[:], in_=by_partition(g)[:, i0:i1, :])
-            g_slot.extend(piece[:, i, :] for i in range(i1 - i0))
+        def load_g(i0, i1, t0, t1):
+            piece = sb.tile([P, i1 - i0, t1 - t0], F32, name=f"g{i0}_{t0}", align_bytes=64)
+            nc.sync.dma_start(out=piece[:], in_=by_partition(g)[:, i0:i1, t0:t1])
+            return piece
+
+        g_low = load_g(0, 2, 0, T)
+        g_high = [load_g(2, PACK, t0, t0 + HALF) for t0 in (0, HALF)]
+
+        def g_at(i, t0, t1):
+            if i < 2:
+                return g_low[:, i, t0:t1]
+            return g_high[t0 // HALF][:, i - 2, :]
 
         deal(w4[:].bitcast(U16), w4_raw[:].bitcast(U16), 8)
         deal(w4_sc[:], w4_sc_raw[:], 16)
 
         for a in range(FIRST_PASS, LAST_W4_PASS):
             src = dy_whole[a]
-            interleave(on_scalar, dy_bf[a][:, :SCALAR_COLS, :], src[:, :, :SCALAR_COLS])
-            interleave(on_vector, dy_bf[a][:, SCALAR_COLS:, :], src[:, :, SCALAR_COLS:])
+            interleave(on_scalar, dy_bf[a][:, :HALF, :], src[:, :, :HALF])
+            interleave(on_vector, dy_bf[a][:, HALF:, :], src[:, :, HALF:])
             if a == 2:
                 deal(w8_sc[:].unsqueeze(1), w8_sc_raw[:].unsqueeze(1), 16)
             quantise_dy(a, 0, T)
@@ -197,20 +202,26 @@ def tile_mix_dyq_fm_pl_mul_kernel(
         deal_w8(w8_rest, 1, PACK)
         products(a, range(1, PACK))
 
-        gate(0, 0, T)
-        store_out(0, 1, 0, T)
-        for h in (slice(0, HALF), slice(HALF, T)):
-            on_scalar(out=sum_1[:, h], in_=acc[1][:, h])
+        def gate_on_gpsimd(i, t0, t1):
+            part = sb.tile([P, t1 - t0], F32, name=f"sum{i}", align_bytes=64)
+            on_scalar(out=part[:], in_=acc[i][:, t0:t1])
             nc.gpsimd.tensor_tensor(
-                out=out_f[:, 1, h], in0=sum_1[:, h], in1=g_slot[1][:, h], op=mybir.AluOpType.mult
+                out=out_f[:, i, t0:t1], in0=part[:], in1=g_low[:, i, t0:t1], op=mybir.AluOpType.mult
             )
+
+        gate(0, 0, HALF)
+        gate_on_gpsimd(0, HALF, T)
+        gate(1, 0, HALF)
+        gate_on_gpsimd(1, HALF, T - QUARTER)
+        store_out(0, 2, 0, HALF)
         for i in range(2, PACK):
             gate(i, 0, HALF)
-        store_out(1, PACK, 0, HALF)
+        store_out(2, PACK, 0, HALF)
         interleave(on_scalar, out_bf[:, :HALF, :], out_f[:, :, :HALF])
+        gate(1, T - QUARTER, T)
         for i in range(2, PACK):
             gate(i, HALF, T)
-        store_out(1, PACK, HALF, T)
+        store_out(0, PACK, HALF, T)
         interleave(on_vector, out_bf[:, HALF:, :], out_f[:, :, HALF:])
         quantise_out(0, HALF)
         store_codes(0, HALF)

@@ -24,6 +24,7 @@ QUADRANTS, SCALE_ROWS = 4, 4
 QUARTER = T // 4
 HALF = T // 2
 RUN = 4
+ALIGN = 256
 W8_PASS, FIRST_PASS, LAST_W4_PASS = 0, 1, PASSES - 1
 
 
@@ -36,30 +37,30 @@ def tile_mix_dyq_fm_pl_mul_kernel(
         ps = ctx.enter_context(tc.psum_pool(name="ps", bufs=1))
         ctx.enter_context(tc.manual_schedule())
 
-        w8_raw = sb.tile([P, D], I32, name="w8_raw", align_bytes=64)
-        w4_raw = sb.tile([P, W4_PASSES, 2 * D], U8, name="w4_raw", align_bytes=64)
-        w4_sc_raw = sb.tile([P, W4_PASSES, D], U8, name="w4_sc_raw", align_bytes=64)
-        w8_sc_raw = sb.tile([P, D], U8, name="w8_sc_raw", align_bytes=64)
-        w8_first = sb.tile([P, 1, P], I32, name="w8_first", align_bytes=64)
-        w8_rest = sb.tile([P, PACK - 1, P], I32, name="w8_rest", align_bytes=64)
+        w8_raw = sb.tile([P, D], I32, name="w8_raw", align_bytes=ALIGN)
+        w4_raw = sb.tile([P, W4_PASSES, 2 * D], U8, name="w4_raw", align_bytes=ALIGN)
+        w4_sc_raw = sb.tile([P, W4_PASSES, D], U8, name="w4_sc_raw", align_bytes=ALIGN)
+        w8_sc_raw = sb.tile([P, D], U8, name="w8_sc_raw", align_bytes=ALIGN)
+        w8_first = sb.tile([P, 1, P], I32, name="w8_first", align_bytes=ALIGN)
+        w8_rest = sb.tile([P, PACK - 1, P], I32, name="w8_rest", align_bytes=ALIGN)
         w8 = [w8_first[:, 0, :]] + [w8_rest[:, i, :] for i in range(PACK - 1)]
-        w8_sc = sb.tile([P, D], U8, name="w8_sc", align_bytes=64)
-        w4 = sb.tile([P, W4_PASSES, 2 * D], U8, name="w4", align_bytes=64)
-        w4_sc = sb.tile([P, W4_PASSES, D], U8, name="w4_sc", align_bytes=64)
-        dy_codes = [sb.tile([P, T], U32, name=f"dy_codes{a}", align_bytes=64) for a in range(PASSES)]
-        dy_sc = [sb.tile([P, T], U8, name=f"dy_sc{a}", align_bytes=64) for a in range(PASSES)]
-        dy_bf = [sb.tile([P, T, PACK], BF16, name=f"dy_bf{a}", align_bytes=64) for a in range(PASSES)]
-        out_codes = sb.tile([P, T], U32, name="out_codes", align_bytes=64)
-        out_sc = sb.tile([P, T], U8, name="out_sc", align_bytes=64)
-        out_f = sb.tile([P, PACK, T], F32, name="out_f", align_bytes=64)
-        out_bf = sb.tile([P, T, PACK], BF16, name="out_bf", align_bytes=64)
+        w8_sc = sb.tile([P, D], U8, name="w8_sc", align_bytes=ALIGN)
+        w4 = sb.tile([P, W4_PASSES, 2 * D], U8, name="w4", align_bytes=ALIGN)
+        w4_sc = sb.tile([P, W4_PASSES, D], U8, name="w4_sc", align_bytes=ALIGN)
+        dy_codes = [sb.tile([P, T], U32, name=f"dy_codes{a}", align_bytes=ALIGN) for a in range(PASSES)]
+        dy_sc = [sb.tile([P, T], U8, name=f"dy_sc{a}", align_bytes=ALIGN) for a in range(PASSES)]
+        dy_bf = [sb.tile([P, T, PACK], BF16, name=f"dy_bf{a}", align_bytes=ALIGN) for a in range(PASSES)]
+        out_codes = sb.tile([P, T], U32, name="out_codes", align_bytes=ALIGN)
+        out_sc = sb.tile([P, T], U8, name="out_sc", align_bytes=ALIGN)
+        out_f = sb.tile([P, PACK, T], F32, name="out_f", align_bytes=ALIGN)
+        out_bf = sb.tile([P, T, PACK], BF16, name="out_bf", align_bytes=ALIGN)
         acc = [ps.tile([P, T], F32, name=f"acc{i}") for i in range(PACK)]
 
         def by_partition(rows):
             return rows.rearrange("(p j) w -> p j w", j=PACK)
 
         def load_dy(a, t0, t1):
-            piece = sb.tile([P, PACK, t1 - t0], F32, name=f"dy{a}_{t0}", align_bytes=64)
+            piece = sb.tile([P, PACK, t1 - t0], F32, name=f"dy{a}_{t0}", align_bytes=ALIGN)
             rows = dy[a * K_PASS : (a + 1) * K_PASS, :]
             nc.sync.dma_start(out=piece[:], in_=by_partition(rows)[:, :, t0:t1])
             return piece
@@ -156,7 +157,7 @@ def tile_mix_dyq_fm_pl_mul_kernel(
         back = load_dy(W8_PASS, T - QUARTER, T)
         nc.sync.dma_start(out=w8_raw[:], in_=w8_words[0].rearrange("p n j -> p (n j)").bitcast(I32))
         def load_g(i0, i1, t0, t1):
-            piece = sb.tile([P, i1 - i0, t1 - t0], F32, name=f"g{i0}_{t0}", align_bytes=64)
+            piece = sb.tile([P, i1 - i0, t1 - t0], F32, name=f"g{i0}_{t0}", align_bytes=ALIGN)
             nc.sync.dma_start(out=piece[:], in_=by_partition(g)[:, i0:i1, t0:t1])
             return piece
 
@@ -203,7 +204,7 @@ def tile_mix_dyq_fm_pl_mul_kernel(
         products(a, range(1, PACK))
 
         def gate_on_gpsimd(i, t0, t1):
-            part = sb.tile([P, t1 - t0], F32, name=f"sum{i}", align_bytes=64)
+            part = sb.tile([P, t1 - t0], F32, name=f"sum{i}", align_bytes=ALIGN)
             on_scalar(out=part[:], in_=acc[i][:, t0:t1])
             nc.gpsimd.tensor_tensor(
                 out=out_f[:, i, t0:t1], in0=part[:], in1=g_low[:, i, t0:t1], op=mybir.AluOpType.mult

@@ -42,8 +42,9 @@ def tile_mix_dyq_fm_pl_mul_kernel(
         w4_sc_raw = sb.tile([P, W4_PASSES, D], U8, name="w4_sc_raw", align_bytes=ALIGN)
         w8_sc_raw = sb.tile([P, D], U8, name="w8_sc_raw", align_bytes=ALIGN)
         w8_first = sb.tile([P, 1, P], I32, name="w8_first", align_bytes=ALIGN)
-        w8_rest = sb.tile([P, PACK - 1, P], I32, name="w8_rest", align_bytes=ALIGN)
-        w8 = [w8_first[:, 0, :]] + [w8_rest[:, i, :] for i in range(PACK - 1)]
+        w8_second = sb.tile([P, 1, P], I32, name="w8_second", align_bytes=ALIGN)
+        w8_rest = sb.tile([P, 2, P], I32, name="w8_rest", align_bytes=ALIGN)
+        w8 = [w8_first[:, 0, :], w8_second[:, 0, :], w8_rest[:, 0, :], w8_rest[:, 1, :]]
         w8_sc = sb.tile([P, D], U8, name="w8_sc", align_bytes=ALIGN)
         w4 = sb.tile([P, W4_PASSES, 2 * D], U8, name="w4", align_bytes=ALIGN)
         w4_sc = sb.tile([P, W4_PASSES, D], U8, name="w4_sc", align_bytes=ALIGN)
@@ -54,7 +55,7 @@ def tile_mix_dyq_fm_pl_mul_kernel(
         out_sc = sb.tile([P, T], U8, name="out_sc", align_bytes=ALIGN)
         out_f = sb.tile([P, PACK, T], F32, name="out_f", align_bytes=ALIGN)
         out_bf = sb.tile([P, T, PACK], BF16, name="out_bf", align_bytes=ALIGN)
-        acc = [ps.tile([P, T], F32, name=f"acc{i}") for i in range(PACK)]
+        acc = [[ps.tile([P, HALF], F32, name=f"acc{i}_{h}") for h in range(2)] for i in range(PACK)]
 
         def by_partition(rows):
             return rows.rearrange("(p j) w -> p j w", j=PACK)
@@ -92,29 +93,35 @@ def tile_mix_dyq_fm_pl_mul_kernel(
                 in_=w8_raw[:].rearrange("p (c m i) -> p c i m", i=PACK, m=RUN)[:, :, i0:i1, :],
             )
 
-        def products(a, slots=range(PACK)):
-            for i in slots:
-                m = slice(i * P, (i + 1) * P)
-                if a == W8_PASS:
-                    lhsT, lhsT_scale = w8[i].bitcast(E4M3), w8_sc[:, m]
-                else:
-                    lhsT = w4[:, a - 1, 2 * i * P : 2 * (i + 1) * P].bitcast(E2M1)
-                    lhsT_scale = w4_sc[:, a - 1, m]
-                nc.tensor.matmul_mx(
-                    out=acc[i][:],
-                    lhsT=lhsT,
-                    lhsT_scale=lhsT_scale,
-                    rhs=dy_codes[a][:].bitcast(E5M2),
-                    rhs_scale=dy_sc[a][:],
-                    start=(a == FIRST_PASS),
-                    stop=(a == W8_PASS),
-                )
+        def product(a, i, h):
+            m, t = slice(i * P, (i + 1) * P), slice(h * HALF, (h + 1) * HALF)
+            if a == W8_PASS:
+                lhsT, lhsT_scale = w8[i].bitcast(E4M3), w8_sc[:, m]
+            else:
+                lhsT = w4[:, a - 1, 2 * i * P : 2 * (i + 1) * P].bitcast(E2M1)
+                lhsT_scale = w4_sc[:, a - 1, m]
+            nc.tensor.matmul_mx(
+                out=acc[i][h][:],
+                lhsT=lhsT,
+                lhsT_scale=lhsT_scale,
+                rhs=dy_codes[a][:, t].bitcast(E5M2),
+                rhs_scale=dy_sc[a][:, t],
+                start=(a == FIRST_PASS),
+                stop=(a == W8_PASS),
+            )
+
+        def products(a):
+            for i in range(PACK):
+                for h in range(2):
+                    product(a, i, h)
 
         def gate(i, t0, t1):
+            h = t0 // HALF
+            t = slice(t0 - h * HALF, t1 - h * HALF)
             nc.vector.tensor_tensor(
                 out=out_f[:, i, t0:t1],
-                in0=acc[i][:, t0:t1],
-                in1=g_at(i, t0, t1),
+                in0=acc[i][h][:, t],
+                in1=g_piece[h][i // 2][:, i % 2, t],
                 op=mybir.AluOpType.mult,
             )
 
@@ -161,13 +168,7 @@ def tile_mix_dyq_fm_pl_mul_kernel(
             nc.sync.dma_start(out=piece[:], in_=by_partition(g)[:, i0:i1, t0:t1])
             return piece
 
-        g_low = load_g(0, 2, 0, T)
-        g_high = [load_g(2, PACK, t0, t0 + HALF) for t0 in (0, HALF)]
-
-        def g_at(i, t0, t1):
-            if i < 2:
-                return g_low[:, i, t0:t1]
-            return g_high[t0 // HALF][:, i - 2, :]
+        g_piece = [[load_g(i, i + 2, t0, t0 + HALF) for i in (0, 2)] for t0 in (0, HALF)]
 
         deal(w4[:].bitcast(U16), w4_raw[:].bitcast(U16), 8)
         deal(w4_sc[:], w4_sc_raw[:], 16)
@@ -192,38 +193,47 @@ def tile_mix_dyq_fm_pl_mul_kernel(
         products(a)
 
         a = W8_PASS
+        SHARE = 96
+        interleave(on_scalar, dy_bf[a][:, :SHARE, :], front[:, :, :SHARE])
+        interleave(on_vector, dy_bf[a][:, SHARE:HALF, :], front[:, :, SHARE:HALF])
         interleave(on_scalar, dy_bf[a][:, HALF : T - QUARTER, :], front[:, :, HALF:])
-        interleave(on_scalar, dy_bf[a][:, T - QUARTER :, :], back[:])
-        interleave(on_vector, dy_bf[a][:, :HALF, :], front[:, :, :HALF])
-        quantise_dy(a, HALF, T - QUARTER)
         quantise_dy(a, 0, HALF)
+        interleave(on_vector, dy_bf[a][:, T - QUARTER :, :], back[:])
         deal_w8(w8_first, 0, 1)
-        quantise_dy(a, T - QUARTER, T)
-        products(a, range(1))
-        deal_w8(w8_rest, 1, PACK)
-        products(a, range(1, PACK))
+        product(a, 0, 0)
+        deal_w8(w8_second, 1, 2)
+        product(a, 1, 0)
+        quantise_dy(a, HALF, T)
+        deal_w8(w8_rest, 2, PACK)
+        product(a, 2, 0)
+        product(a, 3, 0)
+        for i in range(PACK):
+            product(a, i, 1)
 
-        def gate_on_gpsimd(i, t0, t1):
-            part = sb.tile([P, t1 - t0], F32, name=f"sum{i}", align_bytes=ALIGN)
-            on_scalar(out=part[:], in_=acc[i][:, t0:t1])
-            nc.gpsimd.tensor_tensor(
-                out=out_f[:, i, t0:t1], in0=part[:], in1=g_low[:, i, t0:t1], op=mybir.AluOpType.mult
-            )
+        def round_out(copy, t0, t1):
+            interleave(copy, out_bf[:, t0:t1, :], out_f[:, :, t0:t1])
 
+        def gate_high(t0, t1):
+            for i in range(2, PACK):
+                gate(i, t0, t1)
+
+        CUT = HALF + 64
         gate(0, 0, HALF)
-        gate_on_gpsimd(0, HALF, T)
         gate(1, 0, HALF)
-        gate_on_gpsimd(1, HALF, T - QUARTER)
         store_out(0, 2, 0, HALF)
-        for i in range(2, PACK):
-            gate(i, 0, HALF)
+        gate_high(0, QUARTER)
+        round_out(on_scalar, 0, QUARTER)
+        gate_high(QUARTER, HALF)
         store_out(2, PACK, 0, HALF)
-        interleave(on_scalar, out_bf[:, :HALF, :], out_f[:, :, :HALF])
-        gate(1, T - QUARTER, T)
-        for i in range(2, PACK):
-            gate(i, HALF, T)
-        store_out(0, PACK, HALF, T)
-        interleave(on_vector, out_bf[:, HALF:, :], out_f[:, :, HALF:])
+        round_out(on_scalar, QUARTER, HALF)
+        gate(0, HALF, T)
+        gate(1, HALF, T)
+        store_out(0, 2, HALF, T)
+        gate_high(CUT, T)
+        gate_high(HALF, CUT)
+        store_out(2, PACK, HALF, T)
+        round_out(on_scalar, HALF, CUT)
+        round_out(on_vector, CUT, T)
         quantise_out(0, HALF)
         store_codes(0, HALF)
         quantise_out(HALF, T)

@@ -87,10 +87,10 @@ def tile_mix_dyq_fm_pl_mul_kernel(
                 in_=dy_bf[a][:, t0:t1, :].rearrange("p w j -> p (w j)"),
             )
 
-        def deal_w8(dst, i0, i1):
-            nc.vector.tensor_copy(
-                out=dst[:].rearrange("p i (c m) -> p c i m", m=RUN),
-                in_=w8_raw[:].rearrange("p (c m i) -> p c i m", i=PACK, m=RUN)[:, :, i0:i1, :],
+        def deal_w8(copy, dst, i0, i1):
+            copy(
+                out=dst[:].bitcast(U32).rearrange("p i (c m) -> p c i m", m=RUN),
+                in_=w8_raw[:].bitcast(U32).rearrange("p (c m i) -> p c i m", i=PACK, m=RUN)[:, :, i0:i1, :],
             )
 
         def product(a, i, h):
@@ -199,15 +199,16 @@ def tile_mix_dyq_fm_pl_mul_kernel(
         interleave(on_scalar, dy_bf[a][:, HALF : T - QUARTER, :], front[:, :, HALF:])
         quantise_dy(a, 0, HALF)
         interleave(on_vector, dy_bf[a][:, T - QUARTER :, :], back[:])
-        deal_w8(w8_first, 0, 1)
+        deal_w8(on_scalar, w8_rest, 2, PACK)
+        deal_w8(on_vector, w8_first, 0, 1)
         product(a, 0, 0)
-        deal_w8(w8_second, 1, 2)
+        deal_w8(on_vector, w8_second, 1, 2)
         product(a, 1, 0)
         quantise_dy(a, HALF, T)
-        deal_w8(w8_rest, 2, PACK)
+        product(a, 0, 1)
         product(a, 2, 0)
         product(a, 3, 0)
-        for i in range(PACK):
+        for i in range(1, PACK):
             product(a, i, 1)
 
         def round_out(copy, t0, t1):
@@ -218,6 +219,8 @@ def tile_mix_dyq_fm_pl_mul_kernel(
                 gate(i, t0, t1)
 
         CUT = HALF + 64
+        part = sb.tile([P, HALF], F32, name="sum0", align_bytes=ALIGN)
+        on_scalar(out=part[:], in_=acc[0][1][:])
         gate(0, 0, HALF)
         gate(1, 0, HALF)
         store_out(0, 2, 0, HALF)
@@ -226,7 +229,9 @@ def tile_mix_dyq_fm_pl_mul_kernel(
         gate_high(QUARTER, HALF)
         store_out(2, PACK, 0, HALF)
         round_out(on_scalar, QUARTER, HALF)
-        gate(0, HALF, T)
+        nc.gpsimd.tensor_tensor(
+            out=out_f[:, 0, HALF:], in0=part[:], in1=g_piece[1][0][:, 0, :], op=mybir.AluOpType.mult
+        )
         gate(1, HALF, T)
         store_out(0, 2, HALF, T)
         gate_high(CUT, T)

from contextlib import ExitStack

import concourse.mybir as mybir

K, D, T = 2560, 512, 512
FLOPS = 2 * K * D * T

F32 = mybir.dt.float32
BF16 = mybir.dt.bfloat16
I32 = mybir.dt.int32
U32 = mybir.dt.uint32
U16 = mybir.dt.uint16
U8 = mybir.dt.uint8
E4M3 = mybir.dt.float8_e4m3fn_x4
E5M2 = mybir.dt.float8_e5m2_x4
E2M1 = mybir.dt.float4_e2m1fn_x4

P = 128
PACK = 4
K_PASS = P * PACK
PASSES = K // K_PASS
W4_PASSES = PASSES - 1
QUADRANTS, SCALE_ROWS = 4, 4
QUARTER = T // 4
HALF = T // 2
RUN = 4
ALIGN = 256
W8_PASS, FIRST_PASS, LAST_W4_PASS = 0, 1, PASSES - 1


def tile_mix_dyq_fm_pl_mul_kernel(
    tc, dy, w8_words, w8_scales, w4_words, w4_scales, g, out_0, out_1, out_2
):
    nc = tc.nc
    with ExitStack() as ctx:
        sb = ctx.enter_context(tc.tile_pool(name="sb", bufs=1))
        ps = ctx.enter_context(tc.psum_pool(name="ps", bufs=1))
        ctx.enter_context(tc.manual_schedule())

        w8_raw = sb.tile([P, D], I32, name="w8_raw", align_bytes=ALIGN)
        w4_raw = sb.tile([P, W4_PASSES, 2 * D], U8, name="w4_raw", align_bytes=ALIGN)
        w4_sc_raw = sb.tile([P, W4_PASSES, D], U8, name="w4_sc_raw", align_bytes=ALIGN)
        w8_sc_raw = sb.tile([P, D], U8, name="w8_sc_raw", align_bytes=ALIGN)
        w8_first = sb.tile([P, 1, P], I32, name="w8_first", align_bytes=ALIGN)
        w8_second = sb.tile([P, 1, P], I32, name="w8_second", align_bytes=ALIGN)
        w8_rest = sb.tile([P, 2, P], I32, name="w8_rest", align_bytes=ALIGN)
        w8 = [w8_first[:, 0, :], w8_second[:, 0, :], w8_rest[:, 0, :], w8_rest[:, 1, :]]
        w8_sc = sb.tile([P, D], U8, name="w8_sc", align_bytes=ALIGN)
        w4 = sb.tile([P, W4_PASSES, 2 * D], U8, name="w4", align_bytes=ALIGN)
        w4_sc = sb.tile([P, W4_PASSES, D], U8, name="w4_sc", align_bytes=ALIGN)
        dy_codes = [sb.tile([P, T], U32, name=f"dy_codes{a}", align_bytes=ALIGN) for a in range(PASSES)]
        dy_sc = [sb.tile([P, T], U8, name=f"dy_sc{a}", align_bytes=ALIGN) for a in range(PASSES)]
        dy_bf = [sb.tile([P, T, PACK], BF16, name=f"dy_bf{a}", align_bytes=ALIGN) for a in range(PASSES)]
        out_codes = sb.tile([P, T], U32, name="out_codes", align_bytes=ALIGN)
        out_sc = sb.tile([P, T], U8, name="out_sc", align_bytes=ALIGN)
        out_f = sb.tile([P, PACK, T], F32, name="out_f", align_bytes=ALIGN)
        out_bf = sb.tile([P, T, PACK], BF16, name="out_bf", align_bytes=ALIGN)
        acc = [[ps.tile([P, HALF], F32, name=f"acc{i}_{h}") for h in range(2)] for i in range(PACK)]

        def by_partition(rows):
            return rows.rearrange("(p j) w -> p j w", j=PACK)

        def load_dy(a, t0, t1):
            piece = sb.tile([P, PACK, t1 - t0], F32, name=f"dy{a}_{t0}", align_bytes=ALIGN)
            rows = dy[a * K_PASS : (a + 1) * K_PASS, :]
            nc.sync.dma_start(out=piece[:], in_=by_partition(rows)[:, :, t0:t1])
            return piece

        def interleave(copy, dst, src):
            copy(
                out=dst.rearrange("p (c i) j -> p c j i", i=RUN),
                in_=src.rearrange("p j (c i) -> p c j i", i=RUN),
            )

        on_scalar, on_vector = nc.scalar.copy, nc.vector.tensor_copy

        def deal(dst, src, run):
            nc.vector.tensor_copy(
                out=dst.rearrange("p a (i c m) -> p a c i m", i=PACK, m=run),
                in_=src.rearrange("p a (c m i) -> p a c i m", i=PACK, m=run),
            )

        def quantise_dy(a, t0, t1):
            nc.vector.quantize_mx(
                out=dy_codes[a][:, t0:t1].bitcast(E5M2),
                scales=dy_sc[a][:, t0:t1],
                in_=dy_bf[a][:, t0:t1, :].rearrange("p w j -> p (w j)"),
            )

        def deal_w8(copy, dst, i0, i1):
            copy(
                out=dst[:].bitcast(U32).rearrange("p i (c m) -> p c i m", m=RUN),
                in_=w8_raw[:].bitcast(U32).rearrange("p (c m i) -> p c i m", i=PACK, m=RUN)[:, :, i0:i1, :],
            )

        def product(a, i, h):
            m, t = slice(i * P, (i + 1) * P), slice(h * HALF, (h + 1) * HALF)
            if a == W8_PASS:
                lhsT, lhsT_scale = w8[i].bitcast(E4M3), w8_sc[:, m]
            else:
                lhsT = w4[:, a - 1, 2 * i * P : 2 * (i + 1) * P].bitcast(E2M1)
                lhsT_scale = w4_sc[:, a - 1, m]
            nc.tensor.matmul_mx(
                out=acc[i][h][:],
                lhsT=lhsT,
                lhsT_scale=lhsT_scale,
                rhs=dy_codes[a][:, t].bitcast(E5M2),
                rhs_scale=dy_sc[a][:, t],
                start=(a == FIRST_PASS),
                stop=(a == W8_PASS),
            )

        def products(a):
            for i in range(PACK):
                for h in range(2):
                    product(a, i, h)

        def gate(i, t0, t1):
            h = t0 // HALF
            t = slice(t0 - h * HALF, t1 - h * HALF)
            nc.vector.tensor_tensor(
                out=out_f[:, i, t0:t1],
                in0=acc[i][h][:, t],
                in1=g_piece[h][i // 2][:, i % 2, t],
                op=mybir.AluOpType.mult,
            )

        def store_out(i0, i1, t0, t1):
            nc.sync.dma_start(out=by_partition(out_0)[:, i0:i1, t0:t1], in_=out_f[:, i0:i1, t0:t1])

        def quantise_out(t0, t1):
            nc.vector.quantize_mx(
                out=out_codes[:, t0:t1].bitcast(E4M3),
                scales=out_sc[:, t0:t1],
                in_=out_bf[:, t0:t1, :].rearrange("p w j -> p (w j)"),
            )

        def store_codes(t0, t1):
            nc.sync.dma_start(
                out=out_1[0].rearrange("p t i -> p (t i)").bitcast(I32)[:, t0:t1],
                in_=out_codes[:, t0:t1].bitcast(I32),
            )

        nc.vector.memset(w4_sc_raw[:].rearrange("p a n -> p (a n)").bitcast(I32), 0)
        nc.vector.memset(w8_sc_raw[:].bitcast(I32), 0)

        nc.sync.dma_start(
            out=w4_raw[:].bitcast(I32), in_=w4_words.rearrange("a p n -> p a n").bitcast(I32)
        )
        for r in range(SCALE_ROWS):
            nc.sync.dma_start(
                out=w4_sc_raw[r:P:32, :, :].bitcast(I32),
                in_=w4_scales[:, r:16:SCALE_ROWS, :].rearrange("a q n -> q a n").bitcast(I32),
            )
        dy_whole = {FIRST_PASS: load_dy(FIRST_PASS, 0, T)}
        dy_whole[2] = load_dy(2, 0, T)
        for r in range(SCALE_ROWS):
            nc.sync.dma_start(
                out=w8_sc_raw[r:P:32, :].bitcast(I32), in_=w8_scales[0, r:16:SCALE_ROWS, :].bitcast(I32)
            )
        for a in range(3, PASSES):
            dy_whole[a] = load_dy(a, 0, T)
        front = load_dy(W8_PASS, 0, T - QUARTER)
        back = load_dy(W8_PASS, T - QUARTER, T)
        nc.sync.dma_start(out=w8_raw[:], in_=w8_words[0].rearrange("p n j -> p (n j)").bitcast(I32))
        def load_g(i0, i1, t0, t1):
            piece = sb.tile([P, i1 - i0, t1 - t0], F32, name=f"g{i0}_{t0}", align_bytes=ALIGN)
            nc.sync.dma_start(out=piece[:], in_=by_partition(g)[:, i0:i1, t0:t1])
            return piece

        g_piece = [[load_g(i, i + 2, t0, t0 + HALF) for i in (0, 2)] for t0 in (0, HALF)]

        deal(w4[:].bitcast(U16), w4_raw[:].bitcast(U16), 8)
        deal(w4_sc[:], w4_sc_raw[:], 16)

        for a in range(FIRST_PASS, LAST_W4_PASS):
            src = dy_whole[a]
            interleave(on_scalar, dy_bf[a][:, :HALF, :], src[:, :, :HALF])
            interleave(on_vector, dy_bf[a][:, HALF:, :], src[:, :, HALF:])
            if a == 2:
                deal(w8_sc[:].unsqueeze(1), w8_sc_raw[:].unsqueeze(1), 16)
            quantise_dy(a, 0, T)
            products(a)

        a = LAST_W4_PASS
        src = dy_whole[a]
        interleave(on_scalar, dy_bf[a][:, :QUARTER, :], src[:, :, :QUARTER])
        interleave(on_scalar, dy_bf[a][:, QUARTER:HALF, :], src[:, :, QUARTER:HALF])
        interleave(on_vector, dy_bf[a][:, HALF:, :], src[:, :, HALF:])
        quantise_dy(a, 0, QUARTER)
        quantise_dy(a, HALF, T)
        quantise_dy(a, QUARTER, HALF)
        products(a)

        a = W8_PASS
        SHARE = 96
        interleave(on_scalar, dy_bf[a][:, :SHARE, :], front[:, :, :SHARE])
        interleave(on_vector, dy_bf[a][:, SHARE:HALF, :], front[:, :, SHARE:HALF])
        interleave(on_scalar, dy_bf[a][:, HALF : T - QUARTER, :], front[:, :, HALF:])
        quantise_dy(a, 0, HALF)
        interleave(on_vector, dy_bf[a][:, T - QUARTER :, :], back[:])
        deal_w8(on_scalar, w8_rest, 2, PACK)
        deal_w8(on_vector, w8_first, 0, 1)
        product(a, 0, 0)
        deal_w8(on_vector, w8_second, 1, 2)
        product(a, 1, 0)
        quantise_dy(a, HALF, T)
        product(a, 0, 1)
        product(a, 2, 0)
        product(a, 3, 0)
        for i in range(1, PACK):
            product(a, i, 1)

        def round_out(copy, t0, t1):
            interleave(copy, out_bf[:, t0:t1, :], out_f[:, :, t0:t1])

        def gate_high(t0, t1):
            for i in range(2, PACK):
                gate(i, t0, t1)

        CUT = HALF + 64
        part = sb.tile([P, HALF], F32, name="sum0", align_bytes=ALIGN)
        on_scalar(out=part[:], in_=acc[0][1][:])
        gate(0, 0, HALF)
        gate(1, 0, HALF)
        store_out(0, 2, 0, HALF)
        gate_high(0, QUARTER)
        round_out(on_scalar, 0, QUARTER)
        gate_high(QUARTER, HALF)
        store_out(2, PACK, 0, HALF)
        round_out(on_scalar, QUARTER, HALF)
        nc.gpsimd.tensor_tensor(
            out=out_f[:, 0, HALF:], in0=part[:], in1=g_piece[1][0][:, 0, :], op=mybir.AluOpType.mult
        )
        gate(1, HALF, T)
        store_out(0, 2, HALF, T)
        gate_high(CUT, T)
        gate_high(HALF, CUT)
        store_out(2, PACK, HALF, T)
        round_out(on_scalar, HALF, CUT)
        round_out(on_vector, CUT, T)
        quantise_out(0, HALF)
        store_codes(0, HALF)
        quantise_out(HALF, T)
        store_codes(HALF, T)
        for q in range(QUADRANTS):
            queue = nc.scalar if q % 2 == 0 else nc.sync
            queue.dma_start(
                out=out_2[0, SCALE_ROWS * q : SCALE_ROWS * (q + 1), :].bitcast(I32),
                in_=out_sc[32 * q : 32 * q + SCALE_ROWS, :].bitcast(I32),
            )
